import numpy as np
import ml_dtypes


def mxq(x, axis, fmt="e4m3"):
    dtype, down = {"e4m3": (ml_dtypes.float8_e4m3fn, 7), "e5m2": (ml_dtypes.float8_e5m2, 14)}[fmt]
    v = np.moveaxis(np.asarray(x, np.float32).astype(ml_dtypes.bfloat16).astype(np.float64), axis, -1)
    blocks = v.reshape(v.shape[:-1] + (-1, 32))
    amax = np.abs(blocks).max(-1, keepdims=True)
    byte = np.maximum(np.where(amax > 0, np.frexp(amax)[1] - 1 + 127, 0) - down, 1)
    scale = np.exp2(byte - 127.0)
    codes = (blocks / scale).astype(np.float32).astype(dtype).astype(np.float64)
    return np.moveaxis((codes * scale).reshape(v.shape), -1, axis)


WIDE = False


def mx_kscale(k):
    if not WIDE:
        return np.ones(k)
    levels = np.array([10, -10, 5, -5, 0])
    if k % 512:
        return np.exp2(np.random.permutation(np.resize(levels, k // 32))).repeat(32)
    a = np.empty((k // 512, 16))
    for p in range(k // 512):
        a[p, :8] = np.random.permutation(np.resize(levels, 8))
        for g in range(8):
            far = levels[np.abs(levels - a[p, g]) >= 10]
            a[p, g + 8] = far[np.random.randint(len(far))]
    return np.exp2(a.ravel()).repeat(32)


def f64(x):
    return np.asarray(x).astype(np.float64)


def striped(idx):
    return np.tile(idx.reshape(-1, 16).T, (8, 1)).astype(np.uint16)


def unstriped(offs):
    return offs[:16].T.reshape(-1).astype(np.int64)


def sigmoid(v):
    return 1.0 / (1.0 + np.exp(-np.maximum(v, -700.0)))


K, T, S, N, U = 512, 1024, 512, 256, 1024


def setup_inputs():
    n = np.random.standard_normal
    s = mx_kscale(K)[:, None]
    return {
        "xT": (n((K, T)) * s).astype(np.float32),
        "mem": n((N, U)).astype(np.float32),
        "w1": (n((K, N)) / np.sqrt(K) / s).astype(np.float32),
        "w2": (n((K, N)) / np.sqrt(K) / s).astype(np.float32),
        "offs": striped(np.random.permutation(T)[:S]),
        "slot": striped(np.random.permutation(U)[:S]),
    }


def reference(xT, mem, w1, w2, offs, slot):
    old = f64(mem)[:, unstriped(slot)]
    xq = mxq(f64(xT)[:, unstriped(offs)], 0, "e4m3")
    g = sigmoid(mxq(f64(w2), 0, "e4m3").T @ xq)
    y = np.tanh(mxq(f64(w1), 0, "e4m3").T @ xq)
    out = f64(mem).copy()
    out[:, unstriped(slot)] = old + g * (y - old)
    return out

@@ -1,0 +1,159 @@
+from contextlib import ExitStack
+
+import concourse.mybir as mybir
+
+K, T, S, N, U = 512, 1024, 512, 256, 1024
+FLOPS = 2 * 2 * K * N * S
+
+F32 = mybir.dt.float32
+BF16 = mybir.dt.bfloat16
+U32 = mybir.dt.uint32
+U16 = mybir.dt.uint16
+U8 = mybir.dt.uint8
+FP8X4 = mybir.dt.float8_e4m3fn_x4
+ACT = mybir.ActivationFunctionType
+ALU = mybir.AluOpType
+
+P = 128
+PACK = 4
+HALF = S // 2
+LIST_COLS = S // 16
+HALF_COLS = LIST_COLS // 2
+
+
+def tile_picked_gmem_tanh_e_kernel(tc, xT, mem, w1, w2, offs, slot, out):
+    nc = tc.nc
+    with ExitStack() as ctx:
+        sb = ctx.enter_context(tc.tile_pool(name="sb", bufs=1))
+        ps = ctx.enter_context(tc.psum_pool(name="ps", bufs=1))
+
+        warm_in = sb.tile([P, 1], F32, name="warm_in")
+        warm_out = sb.tile([P, 1], F32, name="warm_out")
+        nc.gpsimd.memset(warm_in[:], 0.0)
+        nc.scalar.activation(warm_out[:], warm_in[:], ACT.Sigmoid)
+
+        offs_t = sb.tile([P, LIST_COLS], U16, name="offs_t")
+        slot_t = sb.tile([P, LIST_COLS], U16, name="slot_t")
+        x_planes = xT.rearrange("(p j) t -> p j t", j=PACK)
+        plane = [sb.tile([P, T], F32, name="plane%d" % j) for j in range(PACK)]
+        mem_t = [sb.tile([P, U], F32, name="mem%d" % b) for b in range(2)]
+        w_raw = {}
+        for b in range(2):
+            for m in range(2):
+                w_raw[m, b] = sb.tile([P, PACK, P], F32, name="w_raw%d%d" % (m, b))
+        w_rows = [w.rearrange("(p j) c -> p j c", j=PACK) for w in (w1, w2)]
+
+        def load_w(m, b):
+            nc.sync.dma_start(w_raw[m, b][:], w_rows[m][:, :, b * P : (b + 1) * P])
+
+        nc.sync.dma_start(plane[0][:], x_planes[:, 0, :])
+        nc.sync.dma_start(offs_t[:], offs)
+        for j in range(1, PACK):
+            nc.sync.dma_start(plane[j][:], x_planes[:, j, :])
+        load_w(0, 0)
+        load_w(1, 0)
+        nc.sync.dma_start(slot_t[:], slot)
+        nc.sync.dma_start(mem_t[0][:], mem[0:P, :])
+        load_w(0, 1)
+        load_w(1, 1)
+        nc.sync.dma_start(mem_t[1][:], mem[P : 2 * P, :])
+
+        def half_of(list_tile, h):
+            return list_tile[:, h * HALF_COLS : (h + 1) * HALF_COLS]
+
+        low = sb.tile([P, 2, S], F32, name="low")
+        high = [sb.tile([P, 2, HALF], F32, name="high%d" % h) for h in range(2)]
+        x_bf = [sb.tile([P, HALF, PACK], BF16, name="x_bf%d" % h, align_bytes=64) for h in range(2)]
+        x_codes = sb.tile([P, S], U32, name="x_codes", align_bytes=64)
+        x_scales = sb.tile([P, S], U8, name="x_scales", align_bytes=64)
+
+        for j in range(2):
+            nc.vector.tensor_copy(low[:, j, :], plane[j][:].indirect(offs_t[:]))
+        for h in range(2):
+            nc.scalar.copy(x_bf[h][:, :, 0:2], low[:, :, h * HALF : (h + 1) * HALF].rearrange("p j s -> p s j"))
+        for j in range(2):
+            for h in range(2):
+                nc.vector.tensor_copy(high[h][:, j, :], plane[2 + j][:].indirect(half_of(offs_t, h)))
+
+        w_bf, w_codes, w_scales = {}, {}, {}
+        for key in w_raw:
+            w_bf[key] = sb.tile([P, P, PACK], BF16, name="w_bf%d%d" % key, align_bytes=64)
+            w_codes[key] = sb.tile([P, P], U32, name="w_codes%d%d" % key, align_bytes=64)
+            w_scales[key] = sb.tile([P, P], U8, name="w_scales%d%d" % key, align_bytes=64)
+
+        def quantize_w(key):
+            nc.vector.quantize_mx(
+                out=w_codes[key][:].bitcast(FP8X4),
+                scales=w_scales[key][:],
+                in_=w_bf[key][:].rearrange("p c j -> p (c j)"),
+            )
+
+        def quantize_x(h):
+            cols = slice(h * HALF, (h + 1) * HALF)
+            nc.vector.quantize_mx(
+                out=x_codes[:, cols].bitcast(FP8X4),
+                scales=x_scales[:, cols],
+                in_=x_bf[h][:].rearrange("p s j -> p (s j)"),
+            )
+
+        nc.scalar.copy(x_bf[0][:, :, 2:4], high[0][:].rearrange("p j s -> p s j"))
+        nc.vector.tensor_copy(w_bf[0, 0][:], w_raw[0, 0][:].rearrange("p j c -> p c j"))
+        nc.vector.tensor_copy(x_bf[1][:, :, 2:4], high[1][:].rearrange("p j s -> p s j"))
+        nc.scalar.copy(w_bf[1, 0][:], w_raw[1, 0][:].rearrange("p j c -> p c j"))
+        quantize_w((0, 0))
+        quantize_x(0)
+        quantize_x(1)
+        quantize_w((1, 0))
+
+        cand = [sb.tile([P, S], F32, name="cand%d" % b) for b in range(2)]
+        keep = [sb.tile([P, S], F32, name="keep%d" % b) for b in range(2)]
+        diff = [sb.tile([P, S], F32, name="diff%d" % b) for b in range(2)]
+        kept = [sb.tile([P, S], F32, name="kept%d" % b) for b in range(2)]
+
+        def product(m, b, cols):
+            acc = ps.tile([P, S], F32, name="acc%d%d%d" % (m, b, cols.start))
+            width = cols.stop - cols.start
+            nc.tensor.matmul_mx(
+                out=acc[:, 0:width],
+                lhsT=w_codes[m, b][:].bitcast(FP8X4),
+                lhsT_scale=w_scales[m, b][:],
+                rhs=x_codes[:, cols].bitcast(FP8X4),
+                rhs_scale=x_scales[:, cols],
+                start=True,
+                stop=True,
+            )
+            if m == 0:
+                nc.scalar.activation(cand[b][:, cols], acc[:, 0:width], ACT.Tanh)
+            else:
+                nc.scalar.activation(keep[b][:, cols], acc[:, 0:width], ACT.Sigmoid, scale=-1.0)
+
+        halves = [slice(h * HALF, (h + 1) * HALF) for h in range(2)]
+
+        def blend(b):
+            for h in range(2):
+                nc.vector.tensor_tensor(
+                    diff[b][:, halves[h]], mem_t[b][:].indirect(half_of(slot_t, h)), cand[b][:, halves[h]], ALU.subtract
+                )
+            for h in range(2):
+                nc.vector.tensor_tensor(kept[b][:, halves[h]], diff[b][:, halves[h]], keep[b][:, halves[h]], ALU.mult)
+
+        def scatter(b, h):
+            nc.vector.tensor_tensor(
+                mem_t[b][:].indirect(half_of(slot_t, h)), kept[b][:, halves[h]], cand[b][:, halves[h]], ALU.add
+            )
+
+        for m in range(2):
+            for h in range(2):
+                product(m, 0, halves[h])
+        for m in range(2):
+            nc.scalar.copy(w_bf[m, 1][:], w_raw[m, 1][:].rearrange("p j c -> p c j"))
+        blend(0)
+        for m in range(2):
+            quantize_w((m, 1))
+            product(m, 1, slice(0, S))
+        scatter(0, 0)
+        blend(1)
+        scatter(0, 1)
+        nc.sync.dma_start(out[0:P, :], mem_t[0][:])
+        nc.vector.tensor_tensor(mem_t[1][:].indirect(slot_t[:]), kept[1][:], cand[1][:], ALU.add)
+        nc.sync.dma_start(out[P : 2 * P, :], mem_t[1][:])

@@ -76,12 +76,17 @@ def tile_picked_gmem_tanh_e_kernel(tc, xT, mem, w1, w2, offs, slot, out):
                 nc.vector.tensor_copy(high[h][:, j, :], plane[2 + j][:].indirect(half_of(offs_t, h)))
 
         w_bf, w_codes, w_scales = {}, {}, {}
-        for key in w_raw:
-            w_bf[key] = sb.tile([P, P, PACK], BF16, name="w_bf%d%d" % key, align_bytes=64)
-            w_codes[key] = sb.tile([P, P], U32, name="w_codes%d%d" % key, align_bytes=64)
-            w_scales[key] = sb.tile([P, P], U8, name="w_scales%d%d" % key, align_bytes=64)
+
+        def interleave_w(key, **tag):
+            w_bf[key] = sb.tile([P, P, PACK], BF16, name="w_bf%d%d" % key, align_bytes=64, **tag)
+            nc.scalar.copy(
+                w_bf[key][:].rearrange("p (c i) j -> p c j i", i=4),
+                w_raw[key][:].rearrange("p j (c i) -> p c j i", i=4),
+            )
 
         def quantize_w(key):
+            w_codes[key] = sb.tile([P, P], U32, name="w_codes%d%d" % key, align_bytes=64)
+            w_scales[key] = sb.tile([P, P], U8, name="w_scales%d%d" % key, align_bytes=64)
             nc.vector.quantize_mx(
                 out=w_codes[key][:].bitcast(FP8X4),
                 scales=w_scales[key][:],
@@ -96,10 +101,10 @@ def tile_picked_gmem_tanh_e_kernel(tc, xT, mem, w1, w2, offs, slot, out):
                 in_=x_bf[h][:].rearrange("p s j -> p (s j)"),
             )
 
-        nc.scalar.copy(x_bf[0][:, :, 2:4], high[0][:].rearrange("p j s -> p s j"))
-        nc.vector.tensor_copy(w_bf[0, 0][:], w_raw[0, 0][:].rearrange("p j c -> p c j"))
-        nc.vector.tensor_copy(x_bf[1][:, :, 2:4], high[1][:].rearrange("p j s -> p s j"))
-        nc.scalar.copy(w_bf[1, 0][:], w_raw[1, 0][:].rearrange("p j c -> p c j"))
+        interleave_w((0, 0))
+        interleave_w((1, 0))
+        for h in range(2):
+            nc.vector.tensor_copy(x_bf[h][:, :, 2:4], high[h][:].rearrange("p j s -> p s j"))
         quantize_w((0, 0))
         quantize_x(0)
         quantize_x(1)
@@ -107,7 +112,7 @@ def tile_picked_gmem_tanh_e_kernel(tc, xT, mem, w1, w2, offs, slot, out):
 
         cand = [sb.tile([P, S], F32, name="cand%d" % b) for b in range(2)]
         keep = [sb.tile([P, S], F32, name="keep%d" % b) for b in range(2)]
-        diff = [sb.tile([P, S], F32, name="diff%d" % b) for b in range(2)]
+        diff = {}
         kept = [sb.tile([P, S], F32, name="kept%d" % b) for b in range(2)]
 
         def product(m, b, cols):
@@ -129,11 +134,14 @@ def tile_picked_gmem_tanh_e_kernel(tc, xT, mem, w1, w2, offs, slot, out):
 
         halves = [slice(h * HALF, (h + 1) * HALF) for h in range(2)]
 
-        def blend(b):
+        old = sb.tile([P, S], F32, name="old")
+        nc.vector.tensor_copy(old[:], mem_t[0][:].indirect(slot_t[:]))
+
+        def blend(b, **tag):
+            diff[b] = sb.tile([P, S], F32, name="diff%d" % b, align_bytes=64, **tag)
             for h in range(2):
-                nc.vector.tensor_tensor(
-                    diff[b][:, halves[h]], mem_t[b][:].indirect(half_of(slot_t, h)), cand[b][:, halves[h]], ALU.subtract
-                )
+                before = old[:, halves[h]] if b == 0 else mem_t[b][:].indirect(half_of(slot_t, h))
+                nc.vector.tensor_tensor(diff[b][:, halves[h]], before, cand[b][:, halves[h]], ALU.subtract)
             for h in range(2):
                 nc.vector.tensor_tensor(kept[b][:, halves[h]], diff[b][:, halves[h]], keep[b][:, halves[h]], ALU.mult)
 
@@ -145,14 +153,14 @@ def tile_picked_gmem_tanh_e_kernel(tc, xT, mem, w1, w2, offs, slot, out):
         for m in range(2):
             for h in range(2):
                 product(m, 0, halves[h])
-        for m in range(2):
-            nc.scalar.copy(w_bf[m, 1][:], w_raw[m, 1][:].rearrange("p j c -> p c j"))
+        interleave_w((0, 1), tag="w_codes10")
+        interleave_w((1, 1), tag="w_scales10")
         blend(0)
         for m in range(2):
             quantize_w((m, 1))
             product(m, 1, slice(0, S))
         scatter(0, 0)
-        blend(1)
+        blend(1, tag="w_scales10")
         scatter(0, 1)
         nc.sync.dma_start(out[0:P, :], mem_t[0][:])
         nc.vector.tensor_tensor(mem_t[1][:].indirect(slot_t[:]), kept[1][:], cand[1][:], ALU.add)

@@ -62,7 +62,7 @@ def tile_picked_gmem_tanh_e_kernel(tc, xT, mem, w1, w2, offs, slot, out):
             return list_tile[:, h * HALF_COLS : (h + 1) * HALF_COLS]
 
         low = sb.tile([P, 2, S], F32, name="low")
-        high = [sb.tile([P, 2, HALF], F32, name="high%d" % h) for h in range(2)]
+        high = sb.tile([P, 2, S], F32, name="high")
         x_bf = [sb.tile([P, HALF, PACK], BF16, name="x_bf%d" % h, align_bytes=64) for h in range(2)]
         x_codes = sb.tile([P, S], U32, name="x_codes", align_bytes=64)
         x_scales = sb.tile([P, S], U8, name="x_scales", align_bytes=64)
@@ -71,9 +71,9 @@ def tile_picked_gmem_tanh_e_kernel(tc, xT, mem, w1, w2, offs, slot, out):
             nc.vector.tensor_copy(low[:, j, :], plane[j][:].indirect(offs_t[:]))
         for h in range(2):
             nc.scalar.copy(x_bf[h][:, :, 0:2], low[:, :, h * HALF : (h + 1) * HALF].rearrange("p j s -> p s j"))
-        for j in range(2):
-            for h in range(2):
-                nc.vector.tensor_copy(high[h][:, j, :], plane[2 + j][:].indirect(half_of(offs_t, h)))
+        nc.vector.tensor_copy(high[:, 0, :], plane[2][:].indirect(offs_t[:]))
+        for h in range(2):
+            nc.vector.tensor_copy(high[:, 1, h * HALF : (h + 1) * HALF], plane[3][:].indirect(half_of(offs_t, h)))
 
         w_bf, w_codes, w_scales = {}, {}, {}
 
@@ -104,7 +104,7 @@ def tile_picked_gmem_tanh_e_kernel(tc, xT, mem, w1, w2, offs, slot, out):
         interleave_w((0, 0))
         interleave_w((1, 0))
         for h in range(2):
-            nc.vector.tensor_copy(x_bf[h][:, :, 2:4], high[h][:].rearrange("p j s -> p s j"))
+            nc.vector.tensor_copy(x_bf[h][:, :, 2:4], high[:, :, h * HALF : (h + 1) * HALF].rearrange("p j s -> p s j"))
         quantize_w((0, 0))
         quantize_x(0)
         quantize_x(1)
@@ -135,7 +135,8 @@ def tile_picked_gmem_tanh_e_kernel(tc, xT, mem, w1, w2, offs, slot, out):
         halves = [slice(h * HALF, (h + 1) * HALF) for h in range(2)]
 
         old = sb.tile([P, S], F32, name="old")
-        nc.vector.tensor_copy(old[:], mem_t[0][:].indirect(slot_t[:]))
+        for h in range(2):
+            nc.vector.tensor_copy(old[:, halves[h]], mem_t[0][:].indirect(half_of(slot_t, h)))
 
         def blend(b, **tag):
             diff[b] = sb.tile([P, S], F32, name="diff%d" % b, align_bytes=64, **tag)

@@ -37,83 +37,68 @@ def tile_picked_gmem_tanh_e_kernel(tc, xT, mem, w1, w2, offs, slot, out):
         x_planes = xT.rearrange("(p j) t -> p j t", j=PACK)
         plane = [sb.tile([P, T], F32, name="plane%d" % j) for j in range(PACK)]
         mem_t = [sb.tile([P, U], F32, name="mem%d" % b) for b in range(2)]
-        w_raw = {}
-        for b in range(2):
-            for m in range(2):
-                w_raw[m, b] = sb.tile([P, PACK, P], F32, name="w_raw%d%d" % (m, b))
+        w_raw = [sb.tile([P, PACK, N], F32, name="w_raw%d" % m, align_bytes=64) for m in range(2)]
         w_rows = [w.rearrange("(p j) c -> p j c", j=PACK) for w in (w1, w2)]
-
-        def load_w(m, b):
-            nc.sync.dma_start(w_raw[m, b][:], w_rows[m][:, :, b * P : (b + 1) * P])
 
         nc.sync.dma_start(plane[0][:], x_planes[:, 0, :])
         nc.sync.dma_start(offs_t[:], offs)
         for j in range(1, PACK):
             nc.sync.dma_start(plane[j][:], x_planes[:, j, :])
-        load_w(0, 0)
-        load_w(1, 0)
+        nc.sync.dma_start(w_raw[0][:], w_rows[0])
+        nc.sync.dma_start(w_raw[1][:], w_rows[1])
         nc.sync.dma_start(slot_t[:], slot)
         nc.sync.dma_start(mem_t[0][:], mem[0:P, :])
-        load_w(0, 1)
-        load_w(1, 1)
         nc.sync.dma_start(mem_t[1][:], mem[P : 2 * P, :])
 
         def half_of(list_tile, h):
             return list_tile[:, h * HALF_COLS : (h + 1) * HALF_COLS]
 
-        low = sb.tile([P, 2, S], F32, name="low")
+        halves = [slice(h * HALF, (h + 1) * HALF) for h in range(2)]
+
+        low_bf = [sb.tile([P, T], BF16, name="low_bf%d" % j) for j in range(2)]
         high = sb.tile([P, 2, S], F32, name="high")
-        x_bf = [sb.tile([P, HALF, PACK], BF16, name="x_bf%d" % h, align_bytes=64) for h in range(2)]
-        x_codes = sb.tile([P, S], U32, name="x_codes", align_bytes=64)
+        x_bf = sb.tile([P, S, PACK], BF16, name="x_bf", align_bytes=64)
+        x_codes = sb.tile([P, S], U32, name="x_codes", align_bytes=64, tag="w_raw0")
         x_scales = sb.tile([P, S], U8, name="x_scales", align_bytes=64)
 
         for j in range(2):
-            nc.vector.tensor_copy(low[:, j, :], plane[j][:].indirect(offs_t[:]))
-        for h in range(2):
-            nc.scalar.copy(x_bf[h][:, :, 0:2], low[:, :, h * HALF : (h + 1) * HALF].rearrange("p j s -> p s j"))
+            nc.vector.tensor_copy(low_bf[j][:], plane[j][:])
+            nc.scalar.activation(x_bf[:, :, j], low_bf[j][:].indirect(offs_t[:]), ACT.Copy)
         nc.vector.tensor_copy(high[:, 0, :], plane[2][:].indirect(offs_t[:]))
         for h in range(2):
-            nc.vector.tensor_copy(high[:, 1, h * HALF : (h + 1) * HALF], plane[3][:].indirect(half_of(offs_t, h)))
+            nc.vector.tensor_copy(high[:, 1, halves[h]], plane[3][:].indirect(half_of(offs_t, h)))
+        for h in range(2):
+            nc.vector.tensor_copy(x_bf[:, halves[h], 2:4], high[:, :, halves[h]].rearrange("p j s -> p s j"))
+
+        def quantize_x(h):
+            nc.vector.quantize_mx(
+                out=x_codes[:, halves[h]].bitcast(FP8X4),
+                scales=x_scales[:, halves[h]],
+                in_=x_bf[:, halves[h], :].rearrange("p s j -> p (s j)"),
+            )
 
         w_bf, w_codes, w_scales = {}, {}, {}
 
-        def interleave_w(key, **tag):
-            w_bf[key] = sb.tile([P, P, PACK], BF16, name="w_bf%d%d" % key, align_bytes=64, **tag)
+        def interleave_w(m, b, **tag):
+            w_bf[m, b] = sb.tile([P, P, PACK], BF16, name="w_bf%d%d" % (m, b), align_bytes=64, **tag)
             nc.scalar.copy(
-                w_bf[key][:].rearrange("p (c i) j -> p c j i", i=4),
-                w_raw[key][:].rearrange("p j (c i) -> p c j i", i=4),
+                w_bf[m, b][:].rearrange("p (c i) j -> p c j i", i=4),
+                w_raw[m][:, :, b * P : (b + 1) * P].rearrange("p j (c i) -> p c j i", i=4),
             )
 
-        def quantize_w(key):
-            w_codes[key] = sb.tile([P, P], U32, name="w_codes%d%d" % key, align_bytes=64)
-            w_scales[key] = sb.tile([P, P], U8, name="w_scales%d%d" % key, align_bytes=64)
+        def quantize_w(m, b):
+            w_codes[m, b] = sb.tile([P, P], U32, name="w_codes%d%d" % (m, b), align_bytes=64)
+            w_scales[m, b] = sb.tile([P, P], U8, name="w_scales%d%d" % (m, b), align_bytes=64)
             nc.vector.quantize_mx(
-                out=w_codes[key][:].bitcast(FP8X4),
-                scales=w_scales[key][:],
-                in_=w_bf[key][:].rearrange("p c j -> p (c j)"),
+                out=w_codes[m, b][:].bitcast(FP8X4),
+                scales=w_scales[m, b][:],
+                in_=w_bf[m, b][:].rearrange("p c j -> p (c j)"),
             )
 
-        def quantize_x(h):
-            cols = slice(h * HALF, (h + 1) * HALF)
-            nc.vector.quantize_mx(
-                out=x_codes[:, cols].bitcast(FP8X4),
-                scales=x_scales[:, cols],
-                in_=x_bf[h][:].rearrange("p s j -> p (s j)"),
-            )
-
-        interleave_w((0, 0))
-        interleave_w((1, 0))
-        for h in range(2):
-            nc.vector.tensor_copy(x_bf[h][:, :, 2:4], high[:, :, h * HALF : (h + 1) * HALF].rearrange("p j s -> p s j"))
-        quantize_w((0, 0))
-        quantize_x(0)
-        quantize_x(1)
-        quantize_w((1, 0))
-
-        cand = [sb.tile([P, S], F32, name="cand%d" % b) for b in range(2)]
-        keep = [sb.tile([P, S], F32, name="keep%d" % b) for b in range(2)]
-        diff = {}
-        kept = [sb.tile([P, S], F32, name="kept%d" % b) for b in range(2)]
+        cand = sb.tile([P, 2, S], F32, name="cand")
+        keep = sb.tile([P, 2, S], F32, name="keep")
+        diff = sb.tile([P, 2, S], F32, name="diff")
+        kept = sb.tile([P, 2, S], F32, name="kept")
 
         def product(m, b, cols):
             acc = ps.tile([P, S], F32, name="acc%d%d%d" % (m, b, cols.start))
@@ -128,41 +113,33 @@ def tile_picked_gmem_tanh_e_kernel(tc, xT, mem, w1, w2, offs, slot, out):
                 stop=True,
             )
             if m == 0:
-                nc.scalar.activation(cand[b][:, cols], acc[:, 0:width], ACT.Tanh)
+                nc.scalar.activation(cand[:, b, cols], acc[:, 0:width], ACT.Tanh)
             else:
-                nc.scalar.activation(keep[b][:, cols], acc[:, 0:width], ACT.Sigmoid, scale=-1.0)
+                nc.scalar.activation(keep[:, b, cols], acc[:, 0:width], ACT.Sigmoid, scale=-1.0)
 
-        halves = [slice(h * HALF, (h + 1) * HALF) for h in range(2)]
+        def look_up(b, cols, offsets):
+            nc.vector.tensor_tensor(diff[:, b, cols], mem_t[b][:].indirect(offsets), cand[:, b, cols], ALU.subtract)
 
-        old = sb.tile([P, S], F32, name="old")
+        whole = slice(0, S)
+        interleave_w(0, 0)
+        interleave_w(0, 1)
+        interleave_w(1, 0)
+        quantize_w(0, 0)
         for h in range(2):
-            nc.vector.tensor_copy(old[:, halves[h]], mem_t[0][:].indirect(half_of(slot_t, h)))
-
-        def blend(b, **tag):
-            diff[b] = sb.tile([P, S], F32, name="diff%d" % b, align_bytes=64, **tag)
-            for h in range(2):
-                before = old[:, halves[h]] if b == 0 else mem_t[b][:].indirect(half_of(slot_t, h))
-                nc.vector.tensor_tensor(diff[b][:, halves[h]], before, cand[b][:, halves[h]], ALU.subtract)
-            for h in range(2):
-                nc.vector.tensor_tensor(kept[b][:, halves[h]], diff[b][:, halves[h]], keep[b][:, halves[h]], ALU.mult)
-
-        def scatter(b, h):
-            nc.vector.tensor_tensor(
-                mem_t[b][:].indirect(half_of(slot_t, h)), kept[b][:, halves[h]], cand[b][:, halves[h]], ALU.add
-            )
-
-        for m in range(2):
-            for h in range(2):
-                product(m, 0, halves[h])
-        interleave_w((0, 1), tag="w_codes10")
-        interleave_w((1, 1), tag="w_scales10")
-        blend(0)
-        for m in range(2):
-            quantize_w((m, 1))
-            product(m, 1, slice(0, S))
-        scatter(0, 0)
-        blend(1, tag="w_scales10")
-        scatter(0, 1)
-        nc.sync.dma_start(out[0:P, :], mem_t[0][:])
-        nc.vector.tensor_tensor(mem_t[1][:].indirect(slot_t[:]), kept[1][:], cand[1][:], ALU.add)
-        nc.sync.dma_start(out[P : 2 * P, :], mem_t[1][:])
+            quantize_x(h)
+        quantize_w(0, 1)
+        quantize_w(1, 0)
+        for h in range(2):
+            product(0, 0, halves[h])
+        interleave_w(1, 1, tag="w_codes00")
+        product(0, 1, whole)
+        product(1, 0, whole)
+        for h in range(2):
+            look_up(0, halves[h], half_of(slot_t, h))
+        quantize_w(1, 1)
+        product(1, 1, whole)
+        look_up(1, whole, slot_t[:])
+        nc.vector.tensor_tensor(kept[:], diff[:], keep[:], ALU.mult)
+        for b in range(2):
+            nc.vector.tensor_tensor(mem_t[b][:].indirect(slot_t[:]), kept[:, b, :], cand[:, b, :], ALU.add)
+            nc.sync.dma_start(out[b * P : (b + 1) * P, :], mem_t[b][:])

@@ -8,6 +8,7 @@ FLOPS = 2 * 2 * K * N * S
 F32 = mybir.dt.float32
 BF16 = mybir.dt.bfloat16
 U32 = mybir.dt.uint32
+I32 = mybir.dt.int32
 U16 = mybir.dt.uint16
 U8 = mybir.dt.uint8
 FP8X4 = mybir.dt.float8_e4m3fn_x4
@@ -37,15 +38,23 @@ def tile_picked_gmem_tanh_e_kernel(tc, xT, mem, w1, w2, offs, slot, out):
         x_planes = xT.rearrange("(p j) t -> p j t", j=PACK)
         plane = [sb.tile([P, T], F32, name="plane%d" % j) for j in range(PACK)]
         mem_t = [sb.tile([P, U], F32, name="mem%d" % b) for b in range(2)]
-        w_raw = [sb.tile([P, PACK, N], F32, name="w_raw%d" % m, align_bytes=64) for m in range(2)]
+        w_raw = {}
+        for m in range(2):
+            for b in range(2):
+                w_raw[m, b] = sb.tile([P, PACK, P], F32, name="w_raw%d%d" % (m, b), align_bytes=64)
         w_rows = [w.rearrange("(p j) c -> p j c", j=PACK) for w in (w1, w2)]
+
+        def load_w(m, b):
+            nc.sync.dma_start(w_raw[m, b][:], w_rows[m][:, :, b * P : (b + 1) * P])
 
         nc.sync.dma_start(plane[0][:], x_planes[:, 0, :])
         nc.sync.dma_start(offs_t[:], offs)
         for j in range(1, PACK):
             nc.sync.dma_start(plane[j][:], x_planes[:, j, :])
-        nc.sync.dma_start(w_raw[0][:], w_rows[0])
-        nc.sync.dma_start(w_raw[1][:], w_rows[1])
+        load_w(0, 0)
+        load_w(0, 1)
+        load_w(1, 0)
+        load_w(1, 1)
         nc.sync.dma_start(slot_t[:], slot)
         nc.sync.dma_start(mem_t[0][:], mem[0:P, :])
         nc.sync.dma_start(mem_t[1][:], mem[P : 2 * P, :])
@@ -56,25 +65,29 @@ def tile_picked_gmem_tanh_e_kernel(tc, xT, mem, w1, w2, offs, slot, out):
         halves = [slice(h * HALF, (h + 1) * HALF) for h in range(2)]
 
         low_bf = [sb.tile([P, T], BF16, name="low_bf%d" % j) for j in range(2)]
-        high = sb.tile([P, 2, S], F32, name="high")
-        x_bf = sb.tile([P, S, PACK], BF16, name="x_bf", align_bytes=64)
-        x_codes = sb.tile([P, S], U32, name="x_codes", align_bytes=64, tag="w_raw0")
-        x_scales = sb.tile([P, S], U8, name="x_scales", align_bytes=64)
-
+        pairs = sb.tile([P, 2, S, 2], BF16, name="pairs")
         for j in range(2):
             nc.vector.tensor_copy(low_bf[j][:], plane[j][:])
-            nc.scalar.activation(x_bf[:, :, j], low_bf[j][:].indirect(offs_t[:]), ACT.Copy)
-        nc.vector.tensor_copy(high[:, 0, :], plane[2][:].indirect(offs_t[:]))
-        for h in range(2):
-            nc.vector.tensor_copy(high[:, 1, halves[h]], plane[3][:].indirect(half_of(offs_t, h)))
-        for h in range(2):
-            nc.vector.tensor_copy(x_bf[:, halves[h], 2:4], high[:, :, halves[h]].rearrange("p j s -> p s j"))
+            nc.scalar.activation(pairs[:, 0, :, j], low_bf[j][:].indirect(offs_t[:]), ACT.Copy)
+        for j in range(2):
+            nc.vector.tensor_copy(pairs[:, 1, :, j], plane[2 + j][:].indirect(offs_t[:]))
+        x_bf = {}
+        x_codes = sb.tile([P, S], U32, name="x_codes", align_bytes=64, tag="w_raw01")
+        x_scales = sb.tile([P, S], U8, name="x_scales", align_bytes=64)
+
+        def weave_x(h, tag):
+            x_bf[h] = sb.tile([P, HALF, PACK], BF16, name="x_bf%d" % h, align_bytes=64, tag=tag)
+            words = pairs[:].rearrange("p u s e -> p (u s e)").bitcast(I32).rearrange("p (u s) -> p s u", u=2)
+            nc.vector.tensor_copy(
+                x_bf[h][:].rearrange("p s j -> p (s j)").bitcast(I32).rearrange("p (s u) -> p s u", u=2),
+                words[:, halves[h], :],
+            )
 
         def quantize_x(h):
             nc.vector.quantize_mx(
                 out=x_codes[:, halves[h]].bitcast(FP8X4),
                 scales=x_scales[:, halves[h]],
-                in_=x_bf[:, halves[h], :].rearrange("p s j -> p (s j)"),
+                in_=x_bf[h][:].rearrange("p s j -> p (s j)"),
             )
 
         w_bf, w_codes, w_scales = {}, {}, {}
@@ -83,7 +96,7 @@ def tile_picked_gmem_tanh_e_kernel(tc, xT, mem, w1, w2, offs, slot, out):
             w_bf[m, b] = sb.tile([P, P, PACK], BF16, name="w_bf%d%d" % (m, b), align_bytes=64, **tag)
             nc.scalar.copy(
                 w_bf[m, b][:].rearrange("p (c i) j -> p c j i", i=4),
-                w_raw[m][:, :, b * P : (b + 1) * P].rearrange("p j (c i) -> p c j i", i=4),
+                w_raw[m, b][:].rearrange("p j (c i) -> p c j i", i=4),
             )
 
         def quantize_w(m, b):
@@ -100,11 +113,9 @@ def tile_picked_gmem_tanh_e_kernel(tc, xT, mem, w1, w2, offs, slot, out):
         diff = sb.tile([P, 2, S], F32, name="diff")
         kept = sb.tile([P, 2, S], F32, name="kept")
 
-        def product(m, b, cols):
-            acc = ps.tile([P, S], F32, name="acc%d%d%d" % (m, b, cols.start))
-            width = cols.stop - cols.start
+        def product(acc, m, b, cols):
             nc.tensor.matmul_mx(
-                out=acc[:, 0:width],
+                out=acc,
                 lhsT=w_codes[m, b][:].bitcast(FP8X4),
                 lhsT_scale=w_scales[m, b][:],
                 rhs=x_codes[:, cols].bitcast(FP8X4),
@@ -112,10 +123,18 @@ def tile_picked_gmem_tanh_e_kernel(tc, xT, mem, w1, w2, offs, slot, out):
                 start=True,
                 stop=True,
             )
-            if m == 0:
-                nc.scalar.activation(cand[:, b, cols], acc[:, 0:width], ACT.Tanh)
-            else:
-                nc.scalar.activation(keep[:, b, cols], acc[:, 0:width], ACT.Sigmoid, scale=-1.0)
+
+        def candidate(b, cols):
+            acc = ps.tile([P, S], F32, name="cand_acc%d%d" % (b, cols.start))
+            width = cols.stop - cols.start
+            product(acc[:, 0:width], 0, b, cols)
+            nc.scalar.activation(cand[:, b, cols], acc[:, 0:width], ACT.Tanh)
+
+        def gate(h):
+            acc = ps.tile([P, 2, HALF], F32, name="gate_acc%d" % h)
+            for b in range(2):
+                product(acc[:, b, :], 1, b, halves[h])
+            nc.scalar.activation(keep[:, :, halves[h]], acc[:], ACT.Sigmoid, scale=-1.0)
 
         def look_up(b, cols, offsets):
             nc.vector.tensor_tensor(diff[:, b, cols], mem_t[b][:].indirect(offsets), cand[:, b, cols], ALU.subtract)
@@ -124,22 +143,25 @@ def tile_picked_gmem_tanh_e_kernel(tc, xT, mem, w1, w2, offs, slot, out):
         interleave_w(0, 0)
         interleave_w(0, 1)
         interleave_w(1, 0)
+        interleave_w(1, 1)
         quantize_w(0, 0)
-        for h in range(2):
-            quantize_x(h)
+        weave_x(0, "w_raw00")
         quantize_w(0, 1)
+        quantize_x(0)
+        weave_x(1, "w_raw10")
         quantize_w(1, 0)
-        for h in range(2):
-            product(0, 0, halves[h])
-        interleave_w(1, 1, tag="w_codes00")
-        product(0, 1, whole)
-        product(1, 0, whole)
-        for h in range(2):
-            look_up(0, halves[h], half_of(slot_t, h))
+        quantize_x(1)
         quantize_w(1, 1)
-        product(1, 1, whole)
+        candidate(0, halves[0])
+        candidate(0, halves[1])
+        candidate(1, whole)
+        look_up(0, halves[0], half_of(slot_t, 0))
+        look_up(0, halves[1], half_of(slot_t, 1))
         look_up(1, whole, slot_t[:])
-        nc.vector.tensor_tensor(kept[:], diff[:], keep[:], ALU.mult)
+        for h in range(2):
+            gate(h)
+        for b in range(2):
+            nc.vector.tensor_tensor(kept[:, b, :], diff[:, b, :], keep[:, b, :], ALU.mult)
         for b in range(2):
             nc.vector.tensor_tensor(mem_t[b][:].indirect(slot_t[:]), kept[:, b, :], cand[:, b, :], ALU.add)
             nc.sync.dma_start(out[b * P : (b + 1) * P, :], mem_t[b][:])

@@ -8,7 +8,6 @@ FLOPS = 2 * 2 * K * N * S
 F32 = mybir.dt.float32
 BF16 = mybir.dt.bfloat16
 U32 = mybir.dt.uint32
-I32 = mybir.dt.int32
 U16 = mybir.dt.uint16
 U8 = mybir.dt.uint8
 FP8X4 = mybir.dt.float8_e4m3fn_x4
@@ -38,23 +37,15 @@ def tile_picked_gmem_tanh_e_kernel(tc, xT, mem, w1, w2, offs, slot, out):
         x_planes = xT.rearrange("(p j) t -> p j t", j=PACK)
         plane = [sb.tile([P, T], F32, name="plane%d" % j) for j in range(PACK)]
         mem_t = [sb.tile([P, U], F32, name="mem%d" % b) for b in range(2)]
-        w_raw = {}
-        for m in range(2):
-            for b in range(2):
-                w_raw[m, b] = sb.tile([P, PACK, P], F32, name="w_raw%d%d" % (m, b), align_bytes=64)
+        w_raw = [sb.tile([P, PACK, N], F32, name="w_raw%d" % m, align_bytes=64) for m in range(2)]
         w_rows = [w.rearrange("(p j) c -> p j c", j=PACK) for w in (w1, w2)]
-
-        def load_w(m, b):
-            nc.sync.dma_start(w_raw[m, b][:], w_rows[m][:, :, b * P : (b + 1) * P])
 
         nc.sync.dma_start(plane[0][:], x_planes[:, 0, :])
         nc.sync.dma_start(offs_t[:], offs)
         for j in range(1, PACK):
             nc.sync.dma_start(plane[j][:], x_planes[:, j, :])
-        load_w(0, 0)
-        load_w(0, 1)
-        load_w(1, 0)
-        load_w(1, 1)
+        for m in range(2):
+            nc.sync.dma_start(w_raw[m][:], w_rows[m])
         nc.sync.dma_start(slot_t[:], slot)
         nc.sync.dma_start(mem_t[0][:], mem[0:P, :])
         nc.sync.dma_start(mem_t[1][:], mem[P : 2 * P, :])
@@ -64,24 +55,21 @@ def tile_picked_gmem_tanh_e_kernel(tc, xT, mem, w1, w2, offs, slot, out):
 
         halves = [slice(h * HALF, (h + 1) * HALF) for h in range(2)]
 
-        low_bf = [sb.tile([P, T], BF16, name="low_bf%d" % j) for j in range(2)]
-        pairs = sb.tile([P, 2, S, 2], BF16, name="pairs")
-        for j in range(2):
-            nc.vector.tensor_copy(low_bf[j][:], plane[j][:])
-            nc.scalar.activation(pairs[:, 0, :, j], low_bf[j][:].indirect(offs_t[:]), ACT.Copy)
-        for j in range(2):
-            nc.vector.tensor_copy(pairs[:, 1, :, j], plane[2 + j][:].indirect(offs_t[:]))
-        x_bf = {}
-        x_codes = sb.tile([P, S], U32, name="x_codes", align_bytes=64, tag="w_raw01")
+        low = sb.tile([P, 2, S], F32, name="low")
+        high = sb.tile([P, 2, S], F32, name="high")
+        x_bf = [sb.tile([P, HALF, PACK], BF16, name="x_bf%d" % h, align_bytes=64) for h in range(2)]
+        x_codes = sb.tile([P, S], U32, name="x_codes", align_bytes=64, tag="w_raw0")
         x_scales = sb.tile([P, S], U8, name="x_scales", align_bytes=64)
 
-        def weave_x(h, tag):
-            x_bf[h] = sb.tile([P, HALF, PACK], BF16, name="x_bf%d" % h, align_bytes=64, tag=tag)
-            words = pairs[:].rearrange("p u s e -> p (u s e)").bitcast(I32).rearrange("p (u s) -> p s u", u=2)
-            nc.vector.tensor_copy(
-                x_bf[h][:].rearrange("p s j -> p (s j)").bitcast(I32).rearrange("p (s u) -> p s u", u=2),
-                words[:, halves[h], :],
-            )
+        for j in range(2):
+            nc.vector.tensor_copy(low[:, j, :], plane[j][:].indirect(offs_t[:]))
+        for h in range(2):
+            nc.scalar.copy(x_bf[h][:, :, 0:2], low[:, :, halves[h]].rearrange("p j s -> p s j"))
+        nc.vector.tensor_copy(high[:, 0, :], plane[2][:].indirect(offs_t[:]))
+        for h in range(2):
+            nc.vector.tensor_copy(high[:, 1, halves[h]], plane[3][:].indirect(half_of(offs_t, h)))
+        for h in range(2):
+            nc.vector.tensor_copy(x_bf[h][:, :, 2:4], high[:, :, halves[h]].rearrange("p j s -> p s j"))
 
         def quantize_x(h):
             nc.vector.quantize_mx(
@@ -96,7 +84,7 @@ def tile_picked_gmem_tanh_e_kernel(tc, xT, mem, w1, w2, offs, slot, out):
             w_bf[m, b] = sb.tile([P, P, PACK], BF16, name="w_bf%d%d" % (m, b), align_bytes=64, **tag)
             nc.scalar.copy(
                 w_bf[m, b][:].rearrange("p (c i) j -> p c j i", i=4),
-                w_raw[m, b][:].rearrange("p j (c i) -> p c j i", i=4),
+                w_raw[m][:, :, b * P : (b + 1) * P].rearrange("p j (c i) -> p c j i", i=4),
             )
 
         def quantize_w(m, b):
@@ -145,12 +133,10 @@ def tile_picked_gmem_tanh_e_kernel(tc, xT, mem, w1, w2, offs, slot, out):
         interleave_w(1, 0)
         interleave_w(1, 1)
         quantize_w(0, 0)
-        weave_x(0, "w_raw00")
-        quantize_w(0, 1)
         quantize_x(0)
-        weave_x(1, "w_raw10")
-        quantize_w(1, 0)
         quantize_x(1)
+        quantize_w(0, 1)
+        quantize_w(1, 0)
         quantize_w(1, 1)
         candidate(0, halves[0])
         candidate(0, halves[1])

@@ -19,6 +19,8 @@ PACK = 4
 HALF = S // 2
 LIST_COLS = S // 16
 HALF_COLS = LIST_COLS // 2
+RUN = 4
+CAND, GATE = 0, 1
 
 
 def tile_picked_gmem_tanh_e_kernel(tc, xT, mem, w1, w2, offs, slot, out):
@@ -27,40 +29,36 @@ def tile_picked_gmem_tanh_e_kernel(tc, xT, mem, w1, w2, offs, slot, out):
         sb = ctx.enter_context(tc.tile_pool(name="sb", bufs=1))
         ps = ctx.enter_context(tc.psum_pool(name="ps", bufs=1))
 
-        warm_in = sb.tile([P, 1], F32, name="warm_in")
-        warm_out = sb.tile([P, 1], F32, name="warm_out")
-        nc.gpsimd.memset(warm_in[:], 0.0)
-        nc.scalar.activation(warm_out[:], warm_in[:], ACT.Sigmoid)
+        halves = [slice(h * HALF, (h + 1) * HALF) for h in range(2)]
+        whole = slice(0, S)
+        row_blocks = [slice(b * P, (b + 1) * P) for b in range(2)]
+
+        def half_of(list_tile, h):
+            return list_tile[:, h * HALF_COLS : (h + 1) * HALF_COLS]
 
         offs_t = sb.tile([P, LIST_COLS], U16, name="offs_t")
         slot_t = sb.tile([P, LIST_COLS], U16, name="slot_t")
         x_planes = xT.rearrange("(p j) t -> p j t", j=PACK)
         plane = [sb.tile([P, T], F32, name="plane%d" % j) for j in range(PACK)]
         mem_t = [sb.tile([P, U], F32, name="mem%d" % b) for b in range(2)]
-        w_raw = [sb.tile([P, PACK, N], F32, name="w_raw%d" % m, align_bytes=64) for m in range(2)]
-        w_rows = [w.rearrange("(p j) c -> p j c", j=PACK) for w in (w1, w2)]
+        w_raw = [sb.tile([P, PACK, N], F32, name="w_raw%d" % m, align_bytes=64) for m in (CAND, GATE)]
 
         nc.sync.dma_start(plane[0][:], x_planes[:, 0, :])
         nc.sync.dma_start(offs_t[:], offs)
         for j in range(1, PACK):
             nc.sync.dma_start(plane[j][:], x_planes[:, j, :])
-        for m in range(2):
-            nc.sync.dma_start(w_raw[m][:], w_rows[m])
+        for m, w in ((CAND, w1), (GATE, w2)):
+            nc.sync.dma_start(w_raw[m][:], w.rearrange("(p j) c -> p j c", j=PACK))
         nc.sync.dma_start(slot_t[:], slot)
-        nc.sync.dma_start(mem_t[0][:], mem[0:P, :])
-        nc.sync.dma_start(mem_t[1][:], mem[P : 2 * P, :])
+        for b in range(2):
+            nc.sync.dma_start(mem_t[b][:], mem[row_blocks[b], :])
 
-        def half_of(list_tile, h):
-            return list_tile[:, h * HALF_COLS : (h + 1) * HALF_COLS]
-
-        halves = [slice(h * HALF, (h + 1) * HALF) for h in range(2)]
+        warm_out = sb.tile([P, 1], F32, name="warm_out")
+        nc.scalar.activation(warm_out[:], plane[0][:, 0:1], ACT.Sigmoid)
 
         low = sb.tile([P, 2, S], F32, name="low")
         high = sb.tile([P, 2, S], F32, name="high")
         x_bf = [sb.tile([P, HALF, PACK], BF16, name="x_bf%d" % h, align_bytes=64) for h in range(2)]
-        x_codes = sb.tile([P, S], U32, name="x_codes", align_bytes=64, tag="w_raw0")
-        x_scales = sb.tile([P, S], U8, name="x_scales", align_bytes=64)
-
         for j in range(2):
             nc.vector.tensor_copy(low[:, j, :], plane[j][:].indirect(offs_t[:]))
         for h in range(2):
@@ -71,30 +69,31 @@ def tile_picked_gmem_tanh_e_kernel(tc, xT, mem, w1, w2, offs, slot, out):
         for h in range(2):
             nc.vector.tensor_copy(x_bf[h][:, :, 2:4], high[:, :, halves[h]].rearrange("p j s -> p s j"))
 
-        def quantize_x(h):
-            nc.vector.quantize_mx(
-                out=x_codes[:, halves[h]].bitcast(FP8X4),
-                scales=x_scales[:, halves[h]],
-                in_=x_bf[h][:].rearrange("p s j -> p (s j)"),
-            )
-
         w_bf, w_codes, w_scales = {}, {}, {}
+        for m in (CAND, GATE):
+            for b in range(2):
+                w_bf[m, b] = sb.tile([P, P, PACK], BF16, name="w_bf%d%d" % (m, b), align_bytes=64)
+                nc.scalar.copy(
+                    w_bf[m, b][:].rearrange("p (c i) j -> p c j i", i=RUN),
+                    w_raw[m][:, :, row_blocks[b]].rearrange("p j (c i) -> p c j i", i=RUN),
+                )
 
-        def interleave_w(m, b, **tag):
-            w_bf[m, b] = sb.tile([P, P, PACK], BF16, name="w_bf%d%d" % (m, b), align_bytes=64, **tag)
-            nc.scalar.copy(
-                w_bf[m, b][:].rearrange("p (c i) j -> p c j i", i=4),
-                w_raw[m][:, :, b * P : (b + 1) * P].rearrange("p j (c i) -> p c j i", i=4),
-            )
+        def quantize(codes, scales, values):
+            nc.vector.quantize_mx(out=codes.bitcast(FP8X4), scales=scales, in_=values.rearrange("p c j -> p (c j)"))
 
         def quantize_w(m, b):
             w_codes[m, b] = sb.tile([P, P], U32, name="w_codes%d%d" % (m, b), align_bytes=64)
             w_scales[m, b] = sb.tile([P, P], U8, name="w_scales%d%d" % (m, b), align_bytes=64)
-            nc.vector.quantize_mx(
-                out=w_codes[m, b][:].bitcast(FP8X4),
-                scales=w_scales[m, b][:],
-                in_=w_bf[m, b][:].rearrange("p c j -> p (c j)"),
-            )
+            quantize(w_codes[m, b][:], w_scales[m, b][:], w_bf[m, b][:])
+
+        x_codes = sb.tile([P, S], U32, name="x_codes", align_bytes=64, tag="w_raw0")
+        x_scales = sb.tile([P, S], U8, name="x_scales", align_bytes=64)
+        quantize_w(CAND, 0)
+        for h in range(2):
+            quantize(x_codes[:, halves[h]], x_scales[:, halves[h]], x_bf[h][:])
+        quantize_w(CAND, 1)
+        for b in range(2):
+            quantize_w(GATE, b)
 
         cand = sb.tile([P, 2, S], F32, name="cand")
         keep = sb.tile([P, 2, S], F32, name="keep")
@@ -112,42 +111,24 @@ def tile_picked_gmem_tanh_e_kernel(tc, xT, mem, w1, w2, offs, slot, out):
                 stop=True,
             )
 
-        def candidate(b, cols):
-            acc = ps.tile([P, S], F32, name="cand_acc%d%d" % (b, cols.start))
+        pieces = [(0, halves[h], half_of(slot_t, h)) for h in range(2)] + [(1, whole, slot_t[:])]
+        for b, cols, offsets in pieces:
+            acc = ps.tile([P, S], F32, name="cand_acc%d_%d" % (b, cols.start))
             width = cols.stop - cols.start
-            product(acc[:, 0:width], 0, b, cols)
+            product(acc[:, 0:width], CAND, b, cols)
             nc.scalar.activation(cand[:, b, cols], acc[:, 0:width], ACT.Tanh)
-
-        def gate(h):
-            acc = ps.tile([P, 2, HALF], F32, name="gate_acc%d" % h)
-            for b in range(2):
-                product(acc[:, b, :], 1, b, halves[h])
-            nc.scalar.activation(keep[:, :, halves[h]], acc[:], ACT.Sigmoid, scale=-1.0)
-
-        def look_up(b, cols, offsets):
+        for b, cols, offsets in pieces:
             nc.vector.tensor_tensor(diff[:, b, cols], mem_t[b][:].indirect(offsets), cand[:, b, cols], ALU.subtract)
 
-        whole = slice(0, S)
-        interleave_w(0, 0)
-        interleave_w(0, 1)
-        interleave_w(1, 0)
-        interleave_w(1, 1)
-        quantize_w(0, 0)
-        quantize_x(0)
-        quantize_x(1)
-        quantize_w(0, 1)
-        quantize_w(1, 0)
-        quantize_w(1, 1)
-        candidate(0, halves[0])
-        candidate(0, halves[1])
-        candidate(1, whole)
-        look_up(0, halves[0], half_of(slot_t, 0))
-        look_up(0, halves[1], half_of(slot_t, 1))
-        look_up(1, whole, slot_t[:])
         for h in range(2):
-            gate(h)
+            acc = ps.tile([P, 2, HALF], F32, name="gate_acc%d" % h)
+            for b in range(2):
+                product(acc[:, b, :], GATE, b, halves[h])
+            nc.scalar.activation(keep[:, :, halves[h]], acc[:], ACT.Sigmoid, scale=-1.0)
+
         for b in range(2):
             nc.vector.tensor_tensor(kept[:, b, :], diff[:, b, :], keep[:, b, :], ALU.mult)
+
         for b in range(2):
             nc.vector.tensor_tensor(mem_t[b][:].indirect(slot_t[:]), kept[:, b, :], cand[:, b, :], ALU.add)
-            nc.sync.dma_start(out[b * P : (b + 1) * P, :], mem_t[b][:])
+            nc.sync.dma_start(out[row_blocks[b], :], mem_t[b][:])

@@ -70,13 +70,16 @@ def tile_picked_gmem_tanh_e_kernel(tc, xT, mem, w1, w2, offs, slot, out):
             nc.vector.tensor_copy(x_bf[h][:, :, 2:4], high[:, :, halves[h]].rearrange("p j s -> p s j"))
 
         w_bf, w_codes, w_scales = {}, {}, {}
-        for m in (CAND, GATE):
-            for b in range(2):
-                w_bf[m, b] = sb.tile([P, P, PACK], BF16, name="w_bf%d%d" % (m, b), align_bytes=64)
-                nc.scalar.copy(
-                    w_bf[m, b][:].rearrange("p (c i) j -> p c j i", i=RUN),
-                    w_raw[m][:, :, row_blocks[b]].rearrange("p j (c i) -> p c j i", i=RUN),
-                )
+
+        def interleave_w(copy, m, b, cols):
+            copy(
+                w_bf[m, b][:, cols, :].rearrange("p (c i) j -> p c j i", i=RUN),
+                w_raw[m][:, :, row_blocks[b]][:, :, cols].rearrange("p j (c i) -> p c j i", i=RUN),
+            )
+
+        for m, b in ((CAND, 0), (CAND, 1), (GATE, 0)):
+            w_bf[m, b] = sb.tile([P, P, PACK], BF16, name="w_bf%d%d" % (m, b), align_bytes=64)
+            interleave_w(nc.scalar.copy, m, b, slice(0, P))
 
         def quantize(codes, scales, values):
             nc.vector.quantize_mx(out=codes.bitcast(FP8X4), scales=scales, in_=values.rearrange("p c j -> p (c j)"))
@@ -89,8 +92,13 @@ def tile_picked_gmem_tanh_e_kernel(tc, xT, mem, w1, w2, offs, slot, out):
         x_codes = sb.tile([P, S], U32, name="x_codes", align_bytes=64, tag="w_raw0")
         x_scales = sb.tile([P, S], U8, name="x_scales", align_bytes=64)
         quantize_w(CAND, 0)
-        for h in range(2):
-            quantize(x_codes[:, halves[h]], x_scales[:, halves[h]], x_bf[h][:])
+        quarters = [slice(q * P, (q + 1) * P) for q in range(4)]
+        for q in range(2):
+            quantize(x_codes[:, quarters[q]], x_scales[:, quarters[q]], x_bf[0][:, quarters[q], :])
+        quantize(x_codes[:, halves[1]], x_scales[:, halves[1]], x_bf[1][:])
+        w_bf[GATE, 1] = sb.tile([P, P, PACK], BF16, name="w_bf11", align_bytes=64, tag="x_bf0")
+        interleave_w(nc.scalar.copy, GATE, 1, slice(0, 3 * P // 4))
+        interleave_w(nc.vector.tensor_copy, GATE, 1, slice(3 * P // 4, P))
         quantize_w(CAND, 1)
         for b in range(2):
             quantize_w(GATE, b)
@@ -111,23 +119,26 @@ def tile_picked_gmem_tanh_e_kernel(tc, xT, mem, w1, w2, offs, slot, out):
                 stop=True,
             )
 
-        pieces = [(0, halves[h], half_of(slot_t, h)) for h in range(2)] + [(1, whole, slot_t[:])]
-        for b, cols, offsets in pieces:
+        first_block = [(0, quarters[0]), (0, quarters[1]), (0, halves[1])]
+        for b, cols in first_block + [(1, halves[0]), (1, halves[1])]:
             acc = ps.tile([P, S], F32, name="cand_acc%d_%d" % (b, cols.start))
             width = cols.stop - cols.start
             product(acc[:, 0:width], CAND, b, cols)
             nc.scalar.activation(cand[:, b, cols], acc[:, 0:width], ACT.Tanh)
-        for b, cols, offsets in pieces:
-            nc.vector.tensor_tensor(diff[:, b, cols], mem_t[b][:].indirect(offsets), cand[:, b, cols], ALU.subtract)
+        for b, cols in first_block + [(1, quarters[0]), (1, slice(P, S))]:
+            window = mem_t[b][:].indirect(slot_t[:, cols.start // 16 : cols.stop // 16])
+            nc.vector.tensor_tensor(diff[:, b, cols], window, cand[:, b, cols], ALU.subtract)
 
-        for h in range(2):
-            acc = ps.tile([P, 2, HALF], F32, name="gate_acc%d" % h)
-            for b in range(2):
-                product(acc[:, b, :], GATE, b, halves[h])
-            nc.scalar.activation(keep[:, :, halves[h]], acc[:], ACT.Sigmoid, scale=-1.0)
+        for b, cols in ((0, whole), (1, quarters[0]), (1, slice(P, S))):
+            acc = ps.tile([P, S], F32, name="gate_acc%d_%d" % (b, cols.start))
+            for part in [p for p in (whole, quarters[0], quarters[1], halves[1]) if (p == whole) == (b == 0)]:
+                if cols.start <= part.start and part.stop <= cols.stop:
+                    product(acc[:, part], GATE, b, part)
+            nc.scalar.activation(keep[:, b, cols], acc[:, cols], ACT.Sigmoid, scale=-1.0)
 
-        for b in range(2):
-            nc.vector.tensor_tensor(kept[:, b, :], diff[:, b, :], keep[:, b, :], ALU.mult)
+        flat = [t[:].rearrange("p b s -> p (b s)") for t in (kept, diff, keep)]
+        for cols in (slice(0, S + P), slice(S + P, 2 * S)):
+            nc.vector.tensor_tensor(flat[0][:, cols], flat[1][:, cols], flat[2][:, cols], ALU.mult)
 
         for b in range(2):
             nc.vector.tensor_tensor(mem_t[b][:].indirect(slot_t[:]), kept[:, b, :], cand[:, b, :], ALU.add)

@@ -56,11 +56,13 @@ def tile_picked_gmem_tanh_e_kernel(tc, xT, mem, w1, w2, offs, slot, out):
         warm_out = sb.tile([P, 1], F32, name="warm_out")
         nc.scalar.activation(warm_out[:], plane[0][:, 0:1], ACT.Sigmoid)
 
-        low = sb.tile([P, 2, S], F32, name="low")
+        low = sb.tile([P, 2, S], BF16, name="low")
+        plane0_bf = sb.tile([P, T], BF16, name="plane0_bf")
         high = sb.tile([P, 2, S], F32, name="high")
         x_bf = [sb.tile([P, HALF, PACK], BF16, name="x_bf%d" % h, align_bytes=64) for h in range(2)]
-        for j in range(2):
-            nc.vector.tensor_copy(low[:, j, :], plane[j][:].indirect(offs_t[:]))
+        nc.vector.tensor_copy(plane0_bf[:], plane[0][:])
+        nc.scalar.activation(low[:, 0, :], plane0_bf[:].indirect(offs_t[:]), ACT.Copy)
+        nc.vector.tensor_copy(low[:, 1, :], plane[1][:].indirect(offs_t[:]))
         for h in range(2):
             nc.scalar.copy(x_bf[h][:, :, 0:2], low[:, :, halves[h]].rearrange("p j s -> p s j"))
         nc.vector.tensor_copy(high[:, 0, :], plane[2][:].indirect(offs_t[:]))
@@ -89,13 +91,16 @@ def tile_picked_gmem_tanh_e_kernel(tc, xT, mem, w1, w2, offs, slot, out):
             w_scales[m, b] = sb.tile([P, P], U8, name="w_scales%d%d" % (m, b), align_bytes=64)
             quantize(w_codes[m, b][:], w_scales[m, b][:], w_bf[m, b][:])
 
-        x_codes = sb.tile([P, S], U32, name="x_codes", align_bytes=64, tag="w_raw0")
-        x_scales = sb.tile([P, S], U8, name="x_scales", align_bytes=64)
-        quantize_w(CAND, 0)
         quarters = [slice(q * P, (q + 1) * P) for q in range(4)]
-        for q in range(2):
-            quantize(x_codes[:, quarters[q]], x_scales[:, quarters[q]], x_bf[0][:, quarters[q], :])
-        quantize(x_codes[:, halves[1]], x_scales[:, halves[1]], x_bf[1][:])
+        pieces = [quarters[0], quarters[1], halves[1]]
+        first_codes = sb.tile([P, P], U32, name="first_codes", align_bytes=64)
+        rest_codes = sb.tile([P, S - P], U32, name="rest_codes", align_bytes=64, tag="w_raw0")
+        x_codes = [first_codes[:], rest_codes[:, 0:P], rest_codes[:, P:]]
+        x_scales = sb.tile([P, S], U8, name="x_scales", align_bytes=64)
+        quantize(x_codes[0], x_scales[:, pieces[0]], x_bf[0][:, quarters[0], :])
+        quantize_w(CAND, 0)
+        quantize(x_codes[1], x_scales[:, pieces[1]], x_bf[0][:, quarters[1], :])
+        quantize(x_codes[2], x_scales[:, pieces[2]], x_bf[1][:])
         w_bf[GATE, 1] = sb.tile([P, P, PACK], BF16, name="w_bf11", align_bytes=64, tag="x_bf0")
         interleave_w(nc.scalar.copy, GATE, 1, slice(0, 3 * P // 4))
         interleave_w(nc.vector.tensor_copy, GATE, 1, slice(3 * P // 4, P))
@@ -103,38 +108,35 @@ def tile_picked_gmem_tanh_e_kernel(tc, xT, mem, w1, w2, offs, slot, out):
         for b in range(2):
             quantize_w(GATE, b)
 
-        cand = sb.tile([P, 2, S], F32, name="cand")
+        cand = sb.tile([P, 2, S], F32, name="cand", align_bytes=64, tag="x_bf1")
         keep = sb.tile([P, 2, S], F32, name="keep")
         diff = sb.tile([P, 2, S], F32, name="diff")
         kept = sb.tile([P, 2, S], F32, name="kept")
 
-        def product(acc, m, b, cols):
-            nc.tensor.matmul_mx(
-                out=acc,
-                lhsT=w_codes[m, b][:].bitcast(FP8X4),
-                lhsT_scale=w_scales[m, b][:],
-                rhs=x_codes[:, cols].bitcast(FP8X4),
-                rhs_scale=x_scales[:, cols],
-                start=True,
-                stop=True,
-            )
+        def products(m, b, cols):
+            acc = ps.tile([P, S], F32, name="acc%d%d_%d" % (m, b, cols.start))
+            for codes, piece in zip(x_codes, pieces):
+                if cols.start <= piece.start and piece.stop <= cols.stop:
+                    nc.tensor.matmul_mx(
+                        out=acc[:, piece],
+                        lhsT=w_codes[m, b][:].bitcast(FP8X4),
+                        lhsT_scale=w_scales[m, b][:],
+                        rhs=codes.bitcast(FP8X4),
+                        rhs_scale=x_scales[:, piece],
+                        start=True,
+                        stop=True,
+                    )
+            return acc[:, cols]
 
-        first_block = [(0, quarters[0]), (0, quarters[1]), (0, halves[1])]
+        first_block = [(0, piece) for piece in pieces]
         for b, cols in first_block + [(1, halves[0]), (1, halves[1])]:
-            acc = ps.tile([P, S], F32, name="cand_acc%d_%d" % (b, cols.start))
-            width = cols.stop - cols.start
-            product(acc[:, 0:width], CAND, b, cols)
-            nc.scalar.activation(cand[:, b, cols], acc[:, 0:width], ACT.Tanh)
+            nc.scalar.activation(cand[:, b, cols], products(CAND, b, cols), ACT.Tanh)
         for b, cols in first_block + [(1, quarters[0]), (1, slice(P, S))]:
             window = mem_t[b][:].indirect(slot_t[:, cols.start // 16 : cols.stop // 16])
             nc.vector.tensor_tensor(diff[:, b, cols], window, cand[:, b, cols], ALU.subtract)
 
         for b, cols in ((0, whole), (1, quarters[0]), (1, slice(P, S))):
-            acc = ps.tile([P, S], F32, name="gate_acc%d_%d" % (b, cols.start))
-            for part in [p for p in (whole, quarters[0], quarters[1], halves[1]) if (p == whole) == (b == 0)]:
-                if cols.start <= part.start and part.stop <= cols.stop:
-                    product(acc[:, part], GATE, b, part)
-            nc.scalar.activation(keep[:, b, cols], acc[:, cols], ACT.Sigmoid, scale=-1.0)
+            nc.scalar.activation(keep[:, b, cols], products(GATE, b, cols), ACT.Sigmoid, scale=-1.0)
 
         flat = [t[:].rearrange("p b s -> p (b s)") for t in (kept, diff, keep)]
         for cols in (slice(0, S + P), slice(S + P, 2 * S)):

@@ -102,8 +102,8 @@ def tile_picked_gmem_tanh_e_kernel(tc, xT, mem, w1, w2, offs, slot, out):
         quantize(x_codes[1], x_scales[:, pieces[1]], x_bf[0][:, quarters[1], :])
         quantize(x_codes[2], x_scales[:, pieces[2]], x_bf[1][:])
         w_bf[GATE, 1] = sb.tile([P, P, PACK], BF16, name="w_bf11", align_bytes=64, tag="x_bf0")
-        interleave_w(nc.scalar.copy, GATE, 1, slice(0, 3 * P // 4))
-        interleave_w(nc.vector.tensor_copy, GATE, 1, slice(3 * P // 4, P))
+        interleave_w(nc.scalar.copy, GATE, 1, slice(0, P // 2))
+        interleave_w(nc.vector.tensor_copy, GATE, 1, slice(P // 2, P))
         quantize_w(CAND, 1)
         for b in range(2):
             quantize_w(GATE, b)

@@ -59,17 +59,21 @@ def tile_picked_gmem_tanh_e_kernel(tc, xT, mem, w1, w2, offs, slot, out):
         low = sb.tile([P, 2, S], BF16, name="low")
         plane0_bf = sb.tile([P, T], BF16, name="plane0_bf")
         high = sb.tile([P, 2, S], F32, name="high")
-        x_bf = [sb.tile([P, HALF, PACK], BF16, name="x_bf%d" % h, align_bytes=64) for h in range(2)]
+        quarters = [slice(q * P, (q + 1) * P) for q in range(4)]
+        pieces = [quarters[1], quarters[0], halves[1]]
+        x_bf = [sb.tile([P, c.stop - c.start, PACK], BF16, name="x_bf%d" % i, align_bytes=64) for i, c in enumerate(pieces)]
         nc.vector.tensor_copy(plane0_bf[:], plane[0][:])
         nc.scalar.activation(low[:, 0, :], plane0_bf[:].indirect(offs_t[:]), ACT.Copy)
         nc.vector.tensor_copy(low[:, 1, :], plane[1][:].indirect(offs_t[:]))
-        for h in range(2):
-            nc.scalar.copy(x_bf[h][:, :, 0:2], low[:, :, halves[h]].rearrange("p j s -> p s j"))
+        for i, piece in enumerate(pieces):
+            nc.scalar.copy(x_bf[i][:, :, 0:2], low[:, :, piece].rearrange("p j s -> p s j"))
         nc.vector.tensor_copy(high[:, 0, :], plane[2][:].indirect(offs_t[:]))
-        for h in range(2):
-            nc.vector.tensor_copy(high[:, 1, halves[h]], plane[3][:].indirect(half_of(offs_t, h)))
-        for h in range(2):
-            nc.vector.tensor_copy(x_bf[h][:, :, 2:4], high[:, :, halves[h]].rearrange("p j s -> p s j"))
+        for piece in (quarters[0], quarters[1], halves[1]):
+            nc.vector.tensor_copy(high[:, 1, piece], plane[3][:].indirect(offs_t[:, piece.start // 16 : piece.stop // 16]))
+        high_pairs = high[:].rearrange("p j s -> p s j")
+        nc.gpsimd.tensor_scalar(x_bf[1][:, :, 2:4], high_pairs[:, pieces[1], :], 1.0, 0.0, ALU.mult, ALU.add)
+        for i in (0, 2):
+            nc.vector.tensor_copy(x_bf[i][:, :, 2:4], high_pairs[:, pieces[i], :])
 
         w_bf, w_codes, w_scales = {}, {}, {}
 
@@ -91,24 +95,22 @@ def tile_picked_gmem_tanh_e_kernel(tc, xT, mem, w1, w2, offs, slot, out):
             w_scales[m, b] = sb.tile([P, P], U8, name="w_scales%d%d" % (m, b), align_bytes=64)
             quantize(w_codes[m, b][:], w_scales[m, b][:], w_bf[m, b][:])
 
-        quarters = [slice(q * P, (q + 1) * P) for q in range(4)]
-        pieces = [quarters[0], quarters[1], halves[1]]
         first_codes = sb.tile([P, P], U32, name="first_codes", align_bytes=64)
         rest_codes = sb.tile([P, S - P], U32, name="rest_codes", align_bytes=64, tag="w_raw0")
         x_codes = [first_codes[:], rest_codes[:, 0:P], rest_codes[:, P:]]
         x_scales = sb.tile([P, S], U8, name="x_scales", align_bytes=64)
-        quantize(x_codes[0], x_scales[:, pieces[0]], x_bf[0][:, quarters[0], :])
+        quantize(x_codes[0], x_scales[:, pieces[0]], x_bf[0][:])
         quantize_w(CAND, 0)
-        quantize(x_codes[1], x_scales[:, pieces[1]], x_bf[0][:, quarters[1], :])
-        quantize(x_codes[2], x_scales[:, pieces[2]], x_bf[1][:])
-        w_bf[GATE, 1] = sb.tile([P, P, PACK], BF16, name="w_bf11", align_bytes=64, tag="x_bf0")
+        quantize(x_codes[1], x_scales[:, pieces[1]], x_bf[1][:])
+        quantize(x_codes[2], x_scales[:, pieces[2]], x_bf[2][:])
+        w_bf[GATE, 1] = sb.tile([P, P, PACK], BF16, name="w_bf11", align_bytes=64, tag="x_bf1")
         interleave_w(nc.scalar.copy, GATE, 1, slice(0, P // 2))
         interleave_w(nc.vector.tensor_copy, GATE, 1, slice(P // 2, P))
         quantize_w(CAND, 1)
         for b in range(2):
             quantize_w(GATE, b)
 
-        cand = sb.tile([P, 2, S], F32, name="cand", align_bytes=64, tag="x_bf1")
+        cand = sb.tile([P, 2, S], F32, name="cand", align_bytes=64, tag="x_bf2")
         keep = sb.tile([P, 2, S], F32, name="keep")
         diff = sb.tile([P, 2, S], F32, name="diff")
         kept = sb.tile([P, 2, S], F32, name="kept")

@@ -104,8 +104,7 @@ def tile_picked_gmem_tanh_e_kernel(tc, xT, mem, w1, w2, offs, slot, out):
         quantize(x_codes[1], x_scales[:, pieces[1]], x_bf[1][:])
         quantize(x_codes[2], x_scales[:, pieces[2]], x_bf[2][:])
         w_bf[GATE, 1] = sb.tile([P, P, PACK], BF16, name="w_bf11", align_bytes=64, tag="x_bf1")
-        interleave_w(nc.scalar.copy, GATE, 1, slice(0, P // 2))
-        interleave_w(nc.vector.tensor_copy, GATE, 1, slice(P // 2, P))
+        interleave_w(nc.vector.tensor_copy, GATE, 1, slice(0, P))
         quantize_w(CAND, 1)
         for b in range(2):
             quantize_w(GATE, b)

@@ -18,9 +18,10 @@ P = 128
 PACK = 4
 HALF = S // 2
 LIST_COLS = S // 16
-HALF_COLS = LIST_COLS // 2
 RUN = 4
-CAND, GATE = 0, 1
+X_SCALAR = 192
+OLD_SCALAR = 384
+A, B = 0, 1
 
 
 def tile_picked_gmem_tanh_e_kernel(tc, xT, mem, w1, w2, offs, slot, out):
@@ -29,120 +30,133 @@ def tile_picked_gmem_tanh_e_kernel(tc, xT, mem, w1, w2, offs, slot, out):
         sb = ctx.enter_context(tc.tile_pool(name="sb", bufs=1))
         ps = ctx.enter_context(tc.psum_pool(name="ps", bufs=1))
 
-        halves = [slice(h * HALF, (h + 1) * HALF) for h in range(2)]
+        halves = [slice(0, HALF), slice(HALF, S)]
         whole = slice(0, S)
-        row_blocks = [slice(b * P, (b + 1) * P) for b in range(2)]
+        row_blocks = [slice(b * P, (b + 1) * P) for b in (A, B)]
 
-        def half_of(list_tile, h):
-            return list_tile[:, h * HALF_COLS : (h + 1) * HALF_COLS]
+        def entries(list_tile, cols):
+            return list_tile[:, cols.start // 16 : cols.stop // 16]
 
         offs_t = sb.tile([P, LIST_COLS], U16, name="offs_t")
         slot_t = sb.tile([P, LIST_COLS], U16, name="slot_t")
         x_planes = xT.rearrange("(p j) t -> p j t", j=PACK)
         plane = [sb.tile([P, T], F32, name="plane%d" % j) for j in range(PACK)]
-        mem_t = [sb.tile([P, U], F32, name="mem%d" % b) for b in range(2)]
-        w_raw = [sb.tile([P, PACK, N], F32, name="w_raw%d" % m, align_bytes=64) for m in (CAND, GATE)]
+        mem_t = [sb.tile([P, U], F32, name="mem%d" % b) for b in (A, B)]
+        gate_raw = sb.tile([P, PACK, N], F32, name="gate_raw", align_bytes=64)
+        cand_raw = sb.tile([P, PACK, N], F32, name="cand_raw", align_bytes=64)
 
         nc.sync.dma_start(plane[0][:], x_planes[:, 0, :])
         nc.sync.dma_start(offs_t[:], offs)
         for j in range(1, PACK):
             nc.sync.dma_start(plane[j][:], x_planes[:, j, :])
-        for m, w in ((CAND, w1), (GATE, w2)):
-            nc.sync.dma_start(w_raw[m][:], w.rearrange("(p j) c -> p j c", j=PACK))
+        nc.sync.dma_start(gate_raw[:], w2.rearrange("(p j) c -> p j c", j=PACK))
+        nc.sync.dma_start(cand_raw[:], w1.rearrange("(p j) c -> p j c", j=PACK))
         nc.sync.dma_start(slot_t[:], slot)
-        for b in range(2):
+        for b in (A, B):
             nc.sync.dma_start(mem_t[b][:], mem[row_blocks[b], :])
 
         warm_out = sb.tile([P, 1], F32, name="warm_out")
         nc.scalar.activation(warm_out[:], plane[0][:, 0:1], ACT.Sigmoid)
 
-        low = sb.tile([P, 2, S], BF16, name="low")
-        plane0_bf = sb.tile([P, T], BF16, name="plane0_bf")
-        high = sb.tile([P, 2, S], F32, name="high")
-        quarters = [slice(q * P, (q + 1) * P) for q in range(4)]
-        pieces = [quarters[1], quarters[0], halves[1]]
-        x_bf = [sb.tile([P, c.stop - c.start, PACK], BF16, name="x_bf%d" % i, align_bytes=64) for i, c in enumerate(pieces)]
-        nc.vector.tensor_copy(plane0_bf[:], plane[0][:])
-        nc.scalar.activation(low[:, 0, :], plane0_bf[:].indirect(offs_t[:]), ACT.Copy)
-        nc.vector.tensor_copy(low[:, 1, :], plane[1][:].indirect(offs_t[:]))
-        for i, piece in enumerate(pieces):
-            nc.scalar.copy(x_bf[i][:, :, 0:2], low[:, :, piece].rearrange("p j s -> p s j"))
-        nc.vector.tensor_copy(high[:, 0, :], plane[2][:].indirect(offs_t[:]))
-        for piece in (quarters[0], quarters[1], halves[1]):
-            nc.vector.tensor_copy(high[:, 1, piece], plane[3][:].indirect(offs_t[:, piece.start // 16 : piece.stop // 16]))
-        high_pairs = high[:].rearrange("p j s -> p s j")
-        nc.gpsimd.tensor_scalar(x_bf[1][:, :, 2:4], high_pairs[:, pieces[1], :], 1.0, 0.0, ALU.mult, ALU.add)
-        for i in (0, 2):
-            nc.vector.tensor_copy(x_bf[i][:, :, 2:4], high_pairs[:, pieces[i], :])
+        def scalar_gather(dst, window):
+            nc.scalar.activation(dst, window, ACT.Copy)
 
-        w_bf, w_codes, w_scales = {}, {}, {}
+        picked = [sb.tile([P, 2, S], BF16, name="picked%d" % u) for u in range(2)]
+        x_bf = [sb.tile([P, HALF, PACK], BF16, name="x_bf%d" % h, align_bytes=64) for h in range(2)]
+        scalar_share = slice(0, X_SCALAR)
+        vector_shares = [slice(X_SCALAR, HALF), halves[1]]
 
-        def interleave_w(copy, m, b, cols):
-            copy(
-                w_bf[m, b][:, cols, :].rearrange("p (c i) j -> p c j i", i=RUN),
-                w_raw[m][:, :, row_blocks[b]][:, :, cols].rearrange("p j (c i) -> p c j i", i=RUN),
-            )
+        def interleave_x(copy, u, cols):
+            h = cols.start // HALF
+            dst = x_bf[h][:, cols.start - h * HALF : cols.stop - h * HALF, 2 * u : 2 * u + 2]
+            copy(dst, picked[u][:, :, cols].rearrange("p j s -> p s j"))
 
-        for m, b in ((CAND, 0), (CAND, 1), (GATE, 0)):
-            w_bf[m, b] = sb.tile([P, P, PACK], BF16, name="w_bf%d%d" % (m, b), align_bytes=64)
-            interleave_w(nc.scalar.copy, m, b, slice(0, P))
+        for u in range(2):
+            for j in range(2):
+                window = plane[2 * u + j]
+                scalar_gather(picked[u][:, j, scalar_share], window[:].indirect(entries(offs_t, scalar_share)))
+                if (u, j) == (1, 1):
+                    cuts = [slice(X_SCALAR, X_SCALAR + P), slice(X_SCALAR + P, S)]
+                else:
+                    cuts = [slice(X_SCALAR, S)]
+                for cols in cuts:
+                    nc.vector.tensor_copy(picked[u][:, j, cols], window[:].indirect(entries(offs_t, cols)))
+            interleave_x(nc.scalar.copy, u, scalar_share)
+            for cols in vector_shares:
+                interleave_x(nc.vector.tensor_copy, u, cols)
 
         def quantize(codes, scales, values):
             nc.vector.quantize_mx(out=codes.bitcast(FP8X4), scales=scales, in_=values.rearrange("p c j -> p (c j)"))
 
-        def quantize_w(m, b):
-            w_codes[m, b] = sb.tile([P, P], U32, name="w_codes%d%d" % (m, b), align_bytes=64)
-            w_scales[m, b] = sb.tile([P, P], U8, name="w_scales%d%d" % (m, b), align_bytes=64)
-            quantize(w_codes[m, b][:], w_scales[m, b][:], w_bf[m, b][:])
+        x_codes = [sb.tile([P, HALF], U32, name="x_codes%d" % h, align_bytes=64) for h in range(2)]
+        x_scales = [sb.tile([P, HALF], U8, name="x_scales%d" % h, align_bytes=64) for h in range(2)]
+        for h in range(2):
+            quantize(x_codes[h][:], x_scales[h][:], x_bf[h][:])
 
-        first_codes = sb.tile([P, P], U32, name="first_codes", align_bytes=64)
-        rest_codes = sb.tile([P, S - P], U32, name="rest_codes", align_bytes=64, tag="w_raw0")
-        x_codes = [first_codes[:], rest_codes[:, 0:P], rest_codes[:, P:]]
-        x_scales = sb.tile([P, S], U8, name="x_scales", align_bytes=64)
-        quantize(x_codes[0], x_scales[:, pieces[0]], x_bf[0][:])
-        quantize_w(CAND, 0)
-        quantize(x_codes[1], x_scales[:, pieces[1]], x_bf[1][:])
-        quantize(x_codes[2], x_scales[:, pieces[2]], x_bf[2][:])
-        w_bf[GATE, 1] = sb.tile([P, P, PACK], BF16, name="w_bf11", align_bytes=64, tag="x_bf1")
-        interleave_w(nc.vector.tensor_copy, GATE, 1, slice(0, P))
-        quantize_w(CAND, 1)
-        for b in range(2):
-            quantize_w(GATE, b)
+        def interleave_w(copy, dst, raw, cols):
+            copy(
+                dst.rearrange("p (c i) j -> p c j i", i=RUN),
+                raw[:, :, cols].rearrange("p j (c i) -> p c j i", i=RUN),
+            )
 
-        cand = sb.tile([P, 2, S], F32, name="cand", align_bytes=64, tag="x_bf2")
-        keep = sb.tile([P, 2, S], F32, name="keep")
-        diff = sb.tile([P, 2, S], F32, name="diff")
-        kept = sb.tile([P, 2, S], F32, name="kept")
+        gate_codes, gate_scales = [], []
+        for b in (A, B):
+            gate_bf = sb.tile([P, P, PACK], BF16, name="gate_bf%d" % b, align_bytes=64)
+            interleave_w(nc.scalar.copy, gate_bf[:], gate_raw, row_blocks[b])
+            gate_codes.append(sb.tile([P, P], U32, name="gate_codes%d" % b, align_bytes=64))
+            gate_scales.append(sb.tile([P, P], U8, name="gate_scales%d" % b, align_bytes=64))
+            quantize(gate_codes[b][:], gate_scales[b][:], gate_bf[:])
+        cand_bf = sb.tile([P, N, PACK], BF16, name="cand_bf", align_bytes=64)
+        interleave_w(nc.vector.tensor_copy, cand_bf[:], cand_raw, slice(0, N))
+        cand_codes = sb.tile([P, N], U32, name="cand_codes", align_bytes=64)
+        cand_scales = sb.tile([P, N], U8, name="cand_scales", align_bytes=64)
+        quantize(cand_codes[:], cand_scales[:], cand_bf[:])
 
-        def products(m, b, cols):
-            acc = ps.tile([P, S], F32, name="acc%d%d_%d" % (m, b, cols.start))
-            for codes, piece in zip(x_codes, pieces):
-                if cols.start <= piece.start and piece.stop <= cols.stop:
+        def activate(dst, func, codes, scales, cols, name):
+            acc = ps.tile([P, S], F32, name=name)
+            for h in range(2):
+                if cols.start <= halves[h].start and halves[h].stop <= cols.stop:
                     nc.tensor.matmul_mx(
-                        out=acc[:, piece],
-                        lhsT=w_codes[m, b][:].bitcast(FP8X4),
-                        lhsT_scale=w_scales[m, b][:],
-                        rhs=codes.bitcast(FP8X4),
-                        rhs_scale=x_scales[:, piece],
+                        out=acc[:, halves[h]],
+                        lhsT=codes.bitcast(FP8X4),
+                        lhsT_scale=scales,
+                        rhs=x_codes[h][:].bitcast(FP8X4),
+                        rhs_scale=x_scales[h][:],
                         start=True,
                         stop=True,
                     )
-            return acc[:, cols]
+            nc.scalar.activation(dst[:, cols], acc[:, cols], func, scale=-1.0)
 
-        first_block = [(0, piece) for piece in pieces]
-        for b, cols in first_block + [(1, halves[0]), (1, halves[1])]:
-            nc.scalar.activation(cand[:, b, cols], products(CAND, b, cols), ACT.Tanh)
-        for b, cols in first_block + [(1, quarters[0]), (1, slice(P, S))]:
-            window = mem_t[b][:].indirect(slot_t[:, cols.start // 16 : cols.stop // 16])
-            nc.vector.tensor_tensor(diff[:, b, cols], window, cand[:, b, cols], ALU.subtract)
+        keep = [sb.tile([P, S], F32, name="keep%d" % b) for b in (A, B)]
+        neg_cand = [sb.tile([P, S], F32, name="neg_cand%d" % b) for b in (A, B)]
+        kept = [sb.tile([P, S], F32, name="kept%d" % b) for b in (A, B)]
+        for h in range(2):
+            activate(keep[A], ACT.Sigmoid, gate_codes[A][:], gate_scales[A][:], halves[h], "gate_a%d" % h)
+        activate(keep[B], ACT.Sigmoid, gate_codes[B][:], gate_scales[B][:], whole, "gate_b")
+        for h in range(2):
+            activate(neg_cand[A], ACT.Tanh, cand_codes[:, row_blocks[A]], cand_scales[:, row_blocks[A]], halves[h], "cand_a%d" % h)
+        activate(neg_cand[B], ACT.Tanh, cand_codes[:, row_blocks[B]], cand_scales[:, row_blocks[B]], whole, "cand_b")
 
-        for b, cols in ((0, whole), (1, quarters[0]), (1, slice(P, S))):
-            nc.scalar.activation(keep[:, b, cols], products(GATE, b, cols), ACT.Sigmoid, scale=-1.0)
+        def gated(dst, b, cols):
+            nc.vector.scalar_tensor_tensor(dst[:, cols], keep[b][:, cols], 1.0, neg_cand[b][:, cols], ALU.subtract, ALU.mult)
 
-        flat = [t[:].rearrange("p b s -> p (b s)") for t in (kept, diff, keep)]
-        for cols in (slice(0, S + P), slice(S + P, 2 * S)):
-            nc.vector.tensor_tensor(flat[0][:, cols], flat[1][:, cols], flat[2][:, cols], ALU.mult)
+        def look_up(b, cols):
+            nc.vector.tensor_tensor(kept[b][:, cols], mem_t[b][:].indirect(entries(slot_t, cols)), keep[b][:, cols], ALU.mult)
 
-        for b in range(2):
-            nc.vector.tensor_tensor(mem_t[b][:].indirect(slot_t[:]), kept[:, b, :], cand[:, b, :], ALU.add)
+        new_a = sb.tile([P, S], F32, name="new_a")
+        old_b = sb.tile([P, OLD_SCALAR], F32, name="old_b")
+        for cols in halves:
+            look_up(A, cols)
+        for cols in halves:
+            gated(keep[A], A, cols)
+        scalar_gather(old_b[:], mem_t[B][:].indirect(entries(slot_t, slice(0, OLD_SCALAR))))
+        nc.vector.tensor_tensor(new_a[:, halves[0]], kept[A][:, halves[0]], keep[A][:, halves[0]], ALU.add)
+        gated(neg_cand[A], B, whole)
+        look_up(B, slice(OLD_SCALAR, S))
+        nc.vector.tensor_tensor(kept[B][:, 0:OLD_SCALAR], old_b[:], keep[B][:, 0:OLD_SCALAR], ALU.mult)
+        nc.vector.tensor_tensor(new_a[:, halves[1]], kept[A][:, halves[1]], keep[A][:, halves[1]], ALU.add)
+        for cols in halves:
+            nc.scalar.activation(mem_t[A][:].indirect(entries(slot_t, cols)), new_a[:, cols], ACT.Copy)
+        nc.vector.tensor_tensor(mem_t[B][:].indirect(slot_t[:]), kept[B][:], neg_cand[A][:], ALU.add)
+        for b in (A, B):
             nc.sync.dma_start(out[row_blocks[b], :], mem_t[b][:])

@@ -19,8 +19,9 @@ PACK = 4
 HALF = S // 2
 LIST_COLS = S // 16
 RUN = 4
-X_SCALAR = 192
-OLD_SCALAR = 384
+X_SCALAR = 256
+OLD_SCALAR = 256
+GATE, CAND = 0, 1
 A, B = 0, 1
 
 
@@ -28,6 +29,7 @@ def tile_picked_gmem_tanh_e_kernel(tc, xT, mem, w1, w2, offs, slot, out):
     nc = tc.nc
     with ExitStack() as ctx:
         sb = ctx.enter_context(tc.tile_pool(name="sb", bufs=1))
+        shared = ctx.enter_context(tc.tile_pool(name="shared", bufs=1))
         ps = ctx.enter_context(tc.psum_pool(name="ps", bufs=1))
 
         halves = [slice(0, HALF), slice(HALF, S)]
@@ -61,37 +63,54 @@ def tile_picked_gmem_tanh_e_kernel(tc, xT, mem, w1, w2, offs, slot, out):
         def scalar_gather(dst, window):
             nc.scalar.activation(dst, window, ACT.Copy)
 
-        picked = [sb.tile([P, 2, S], BF16, name="picked%d" % u) for u in range(2)]
         x_bf = [sb.tile([P, HALF, PACK], BF16, name="x_bf%d" % h, align_bytes=64) for h in range(2)]
-        scalar_share = slice(0, X_SCALAR)
-        vector_shares = [slice(X_SCALAR, HALF), halves[1]]
+        x_vector = S - X_SCALAR
+        vector_shares = [slice(0, P), slice(P, x_vector)]
+        block_bytes = P * PACK * 2
 
-        def interleave_x(copy, u, cols):
+        def interleave_x(copy, u, cols, src):
             h = cols.start // HALF
             dst = x_bf[h][:, cols.start - h * HALF : cols.stop - h * HALF, 2 * u : 2 * u + 2]
-            copy(dst, picked[u][:, :, cols].rearrange("p j s -> p s j"))
+            copy(dst, src.rearrange("p j s -> p s j"))
 
-        for u in range(2):
-            for j in range(2):
-                window = plane[2 * u + j]
-                scalar_gather(picked[u][:, j, scalar_share], window[:].indirect(entries(offs_t, scalar_share)))
-                if (u, j) == (1, 1):
-                    cuts = [slice(X_SCALAR, X_SCALAR + P), slice(X_SCALAR + P, S)]
-                else:
-                    cuts = [slice(X_SCALAR, S)]
-                for cols in cuts:
-                    nc.vector.tensor_copy(picked[u][:, j, cols], window[:].indirect(entries(offs_t, cols)))
-            interleave_x(nc.scalar.copy, u, scalar_share)
-            for cols in vector_shares:
-                interleave_x(nc.vector.tensor_copy, u, cols)
+        scalar_shares = [slice(x_vector, x_vector + P), slice(x_vector + P, S)]
+
+        left = []
+
+        def picked_tiles(name, cuts, base):
+            first, second = (c.stop - c.start for c in cuts)
+            low = [
+                shared.tile([P, 2, first], BF16, name=name + "_low0", offset=base, align_bytes=64),
+                sb.tile([P, 2, second], BF16, name=name + "_low1"),
+            ]
+            high = [
+                shared.tile([P, 2, first], BF16, name=name + "_high0", offset=base - 2 * first, align_bytes=64),
+                shared.tile([P, 2, second], BF16, name=name + "_high1", offset=base + 2 * first, align_bytes=64),
+            ]
+            return low, high
+
+        for gather, copy, cuts, name, base in (
+            (scalar_gather, nc.scalar.copy, scalar_shares, "s", 4 * block_bytes),
+            (nc.vector.tensor_copy, nc.vector.tensor_copy, vector_shares, "v", 3 * block_bytes // 2),
+        ):
+            for u, pair in enumerate(picked_tiles(name, cuts, base)):
+                for j in range(2):
+                    for picked, cols in zip(pair, cuts):
+                        gather(picked[:, j, :], plane[2 * u + j][:].indirect(entries(offs_t, cols)))
+                for picked, cols in zip(pair, cuts):
+                    if (u, cols) == (1, scalar_shares[1]):
+                        left.append((cols, picked))
+                    else:
+                        interleave_x(copy, u, cols, picked[:])
+
+        for cols, picked in left:
+            interleave_x(nc.vector.tensor_copy, 1, cols, picked[:])
 
         def quantize(codes, scales, values):
             nc.vector.quantize_mx(out=codes.bitcast(FP8X4), scales=scales, in_=values.rearrange("p c j -> p (c j)"))
 
         x_codes = [sb.tile([P, HALF], U32, name="x_codes%d" % h, align_bytes=64) for h in range(2)]
         x_scales = [sb.tile([P, HALF], U8, name="x_scales%d" % h, align_bytes=64) for h in range(2)]
-        for h in range(2):
-            quantize(x_codes[h][:], x_scales[h][:], x_bf[h][:])
 
         def interleave_w(copy, dst, raw, cols):
             copy(
@@ -99,18 +118,27 @@ def tile_picked_gmem_tanh_e_kernel(tc, xT, mem, w1, w2, offs, slot, out):
                 raw[:, :, cols].rearrange("p j (c i) -> p c j i", i=RUN),
             )
 
-        gate_codes, gate_scales = [], []
+        w_codes, w_scales = {}, {}
+        quantize(x_codes[0][:], x_scales[0][:], x_bf[0][:])
+        gate_bf = []
         for b in (A, B):
-            gate_bf = sb.tile([P, P, PACK], BF16, name="gate_bf%d" % b, align_bytes=64)
-            interleave_w(nc.scalar.copy, gate_bf[:], gate_raw, row_blocks[b])
-            gate_codes.append(sb.tile([P, P], U32, name="gate_codes%d" % b, align_bytes=64))
-            gate_scales.append(sb.tile([P, P], U8, name="gate_scales%d" % b, align_bytes=64))
-            quantize(gate_codes[b][:], gate_scales[b][:], gate_bf[:])
-        cand_bf = sb.tile([P, N, PACK], BF16, name="cand_bf", align_bytes=64)
-        interleave_w(nc.vector.tensor_copy, cand_bf[:], cand_raw, slice(0, N))
-        cand_codes = sb.tile([P, N], U32, name="cand_codes", align_bytes=64)
-        cand_scales = sb.tile([P, N], U8, name="cand_scales", align_bytes=64)
-        quantize(cand_codes[:], cand_scales[:], cand_bf[:])
+            gate_bf.append(shared.tile([P, P, PACK], BF16, name="gate_bf%d" % b, offset=(1 + 3 * b) * block_bytes // 2, align_bytes=64))
+            interleave_w(nc.scalar.copy, gate_bf[b][:], gate_raw, row_blocks[b])
+            w_codes[GATE, b] = sb.tile([P, P], U32, name="gate_codes%d" % b, align_bytes=64)
+            w_scales[GATE, b] = sb.tile([P, P], U8, name="gate_scales%d" % b, align_bytes=64)
+        quantize(w_codes[GATE, A][:], w_scales[GATE, A][:], gate_bf[A][:])
+        quantize(x_codes[1][:], x_scales[1][:], x_bf[1][:])
+        cand_bf = []
+        for b in (A, B):
+            cand_bf.append(shared.tile([P, P, PACK], BF16, name="cand_bf%d" % b, offset=b * block_bytes, align_bytes=64))
+            interleave_w(nc.vector.tensor_copy, cand_bf[b][:], cand_raw, row_blocks[b])
+            if b == A:
+                quantize(w_codes[GATE, B][:], w_scales[GATE, B][:], gate_bf[B][:])
+        for b in (A, B):
+            cand_codes = sb.tile([P, P], U32, name="cand_codes%d" % b, align_bytes=64)
+            cand_scales = sb.tile([P, P], U8, name="cand_scales%d" % b, align_bytes=64)
+            quantize(cand_codes[:], cand_scales[:], cand_bf[b][:])
+            w_codes[CAND, b], w_scales[CAND, b] = cand_codes[:], cand_scales[:]
 
         def activate(dst, func, codes, scales, cols, name):
             acc = ps.tile([P, S], F32, name=name)
@@ -131,11 +159,11 @@ def tile_picked_gmem_tanh_e_kernel(tc, xT, mem, w1, w2, offs, slot, out):
         neg_cand = [sb.tile([P, S], F32, name="neg_cand%d" % b) for b in (A, B)]
         kept = [sb.tile([P, S], F32, name="kept%d" % b) for b in (A, B)]
         for h in range(2):
-            activate(keep[A], ACT.Sigmoid, gate_codes[A][:], gate_scales[A][:], halves[h], "gate_a%d" % h)
-        activate(keep[B], ACT.Sigmoid, gate_codes[B][:], gate_scales[B][:], whole, "gate_b")
-        for h in range(2):
-            activate(neg_cand[A], ACT.Tanh, cand_codes[:, row_blocks[A]], cand_scales[:, row_blocks[A]], halves[h], "cand_a%d" % h)
-        activate(neg_cand[B], ACT.Tanh, cand_codes[:, row_blocks[B]], cand_scales[:, row_blocks[B]], whole, "cand_b")
+            activate(keep[A], ACT.Sigmoid, w_codes[GATE, A][:], w_scales[GATE, A][:], halves[h], "gate_a%d" % h)
+        activate(keep[B], ACT.Sigmoid, w_codes[GATE, B][:], w_scales[GATE, B][:], whole, "gate_b")
+        for b in (A, B):
+            for h in range(2):
+                activate(neg_cand[b], ACT.Tanh, w_codes[CAND, b], w_scales[CAND, b], halves[h], "cand%d%d" % (b, h))
 
         def gated(dst, b, cols):
             nc.vector.scalar_tensor_tensor(dst[:, cols], keep[b][:, cols], 1.0, neg_cand[b][:, cols], ALU.subtract, ALU.mult)

@@ -158,9 +158,9 @@ def tile_picked_gmem_tanh_e_kernel(tc, xT, mem, w1, w2, offs, slot, out):
         keep = [sb.tile([P, S], F32, name="keep%d" % b) for b in (A, B)]
         neg_cand = [sb.tile([P, S], F32, name="neg_cand%d" % b) for b in (A, B)]
         kept = [sb.tile([P, S], F32, name="kept%d" % b) for b in (A, B)]
-        for h in range(2):
-            activate(keep[A], ACT.Sigmoid, w_codes[GATE, A][:], w_scales[GATE, A][:], halves[h], "gate_a%d" % h)
-        activate(keep[B], ACT.Sigmoid, w_codes[GATE, B][:], w_scales[GATE, B][:], whole, "gate_b")
+        for b in (A, B):
+            for h in range(2):
+                activate(keep[b], ACT.Sigmoid, w_codes[GATE, b][:], w_scales[GATE, b][:], halves[h], "gate%d%d" % (b, h))
         for b in (A, B):
             for h in range(2):
                 activate(neg_cand[b], ACT.Tanh, w_codes[CAND, b], w_scales[CAND, b], halves[h], "cand%d%d" % (b, h))
@@ -186,5 +186,5 @@ def tile_picked_gmem_tanh_e_kernel(tc, xT, mem, w1, w2, offs, slot, out):
         for cols in halves:
             nc.scalar.activation(mem_t[A][:].indirect(entries(slot_t, cols)), new_a[:, cols], ACT.Copy)
         nc.vector.tensor_tensor(mem_t[B][:].indirect(slot_t[:]), kept[B][:], neg_cand[A][:], ALU.add)
-        for b in (A, B):
-            nc.sync.dma_start(out[row_blocks[b], :], mem_t[b][:])
+        nc.scalar.dma_start(out[row_blocks[A], :], mem_t[A][:])
+        nc.sync.dma_start(out[row_blocks[B], :], mem_t[B][:])

from contextlib import ExitStack

import concourse.mybir as mybir

K, T, S, N, U = 512, 1024, 512, 256, 1024
FLOPS = 2 * 2 * K * N * S

F32 = mybir.dt.float32
BF16 = mybir.dt.bfloat16
U32 = mybir.dt.uint32
U16 = mybir.dt.uint16
U8 = mybir.dt.uint8
FP8X4 = mybir.dt.float8_e4m3fn_x4
ACT = mybir.ActivationFunctionType
ALU = mybir.AluOpType

P = 128
PACK = 4
HALF = S // 2
LIST_COLS = S // 16
RUN = 4
X_SCALAR = 256
OLD_SCALAR = 256
GATE, CAND = 0, 1
A, B = 0, 1


def tile_picked_gmem_tanh_e_kernel(tc, xT, mem, w1, w2, offs, slot, out):
    nc = tc.nc
    with ExitStack() as ctx:
        sb = ctx.enter_context(tc.tile_pool(name="sb", bufs=1))
        shared = ctx.enter_context(tc.tile_pool(name="shared", bufs=1))
        ps = ctx.enter_context(tc.psum_pool(name="ps", bufs=1))

        halves = [slice(0, HALF), slice(HALF, S)]
        whole = slice(0, S)
        row_blocks = [slice(b * P, (b + 1) * P) for b in (A, B)]

        def entries(list_tile, cols):
            return list_tile[:, cols.start // 16 : cols.stop // 16]

        offs_t = sb.tile([P, LIST_COLS], U16, name="offs_t")
        slot_t = sb.tile([P, LIST_COLS], U16, name="slot_t")
        x_planes = xT.rearrange("(p j) t -> p j t", j=PACK)
        plane = [sb.tile([P, T], F32, name="plane%d" % j) for j in range(PACK)]
        mem_t = [sb.tile([P, U], F32, name="mem%d" % b) for b in (A, B)]
        gate_raw = sb.tile([P, PACK, N], F32, name="gate_raw", align_bytes=64)
        cand_raw = sb.tile([P, PACK, N], F32, name="cand_raw", align_bytes=64)

        nc.sync.dma_start(plane[0][:], x_planes[:, 0, :])
        nc.sync.dma_start(offs_t[:], offs)
        for j in range(1, PACK):
            nc.sync.dma_start(plane[j][:], x_planes[:, j, :])
        nc.sync.dma_start(gate_raw[:], w2.rearrange("(p j) c -> p j c", j=PACK))
        nc.sync.dma_start(cand_raw[:], w1.rearrange("(p j) c -> p j c", j=PACK))
        nc.sync.dma_start(slot_t[:], slot)
        for b in (A, B):
            nc.sync.dma_start(mem_t[b][:], mem[row_blocks[b], :])

        warm_out = sb.tile([P, 1], F32, name="warm_out")
        nc.scalar.activation(warm_out[:], plane[0][:, 0:1], ACT.Sigmoid)

        def scalar_gather(dst, window):
            nc.scalar.activation(dst, window, ACT.Copy)

        x_bf = [sb.tile([P, HALF, PACK], BF16, name="x_bf%d" % h, align_bytes=64) for h in range(2)]
        x_vector = S - X_SCALAR
        vector_shares = [slice(0, P), slice(P, x_vector)]
        block_bytes = P * PACK * 2

        def interleave_x(copy, u, cols, src):
            h = cols.start // HALF
            dst = x_bf[h][:, cols.start - h * HALF : cols.stop - h * HALF, 2 * u : 2 * u + 2]
            copy(dst, src.rearrange("p j s -> p s j"))

        scalar_shares = [slice(x_vector, x_vector + P), slice(x_vector + P, S)]

        left = []

        def picked_tiles(name, cuts, base):
            first, second = (c.stop - c.start for c in cuts)
            low = [
                shared.tile([P, 2, first], BF16, name=name + "_low0", offset=base, align_bytes=64),
                sb.tile([P, 2, second], BF16, name=name + "_low1"),
            ]
            high = [
                shared.tile([P, 2, first], BF16, name=name + "_high0", offset=base - 2 * first, align_bytes=64),
                shared.tile([P, 2, second], BF16, name=name + "_high1", offset=base + 2 * first, align_bytes=64),
            ]
            return low, high

        for gather, copy, cuts, name, base in (
            (scalar_gather, nc.scalar.copy, scalar_shares, "s", 4 * block_bytes),
            (nc.vector.tensor_copy, nc.vector.tensor_copy, vector_shares, "v", 3 * block_bytes // 2),
        ):
            for u, pair in enumerate(picked_tiles(name, cuts, base)):
                for j in range(2):
                    for picked, cols in zip(pair, cuts):
                        gather(picked[:, j, :], plane[2 * u + j][:].indirect(entries(offs_t, cols)))
                for picked, cols in zip(pair, cuts):
                    if (u, cols) == (1, scalar_shares[1]):
                        left.append((cols, picked))
                    else:
                        interleave_x(copy, u, cols, picked[:])

        for cols, picked in left:
            interleave_x(nc.vector.tensor_copy, 1, cols, picked[:])

        def quantize(codes, scales, values):
            nc.vector.quantize_mx(out=codes.bitcast(FP8X4), scales=scales, in_=values.rearrange("p c j -> p (c j)"))

        x_codes = [sb.tile([P, HALF], U32, name="x_codes%d" % h, align_bytes=64) for h in range(2)]
        x_scales = [sb.tile([P, HALF], U8, name="x_scales%d" % h, align_bytes=64) for h in range(2)]

        def interleave_w(copy, dst, raw, cols):
            copy(
                dst.rearrange("p (c i) j -> p c j i", i=RUN),
                raw[:, :, cols].rearrange("p j (c i) -> p c j i", i=RUN),
            )

        w_codes, w_scales = {}, {}
        quantize(x_codes[0][:], x_scales[0][:], x_bf[0][:])
        gate_bf = []
        for b in (A, B):
            gate_bf.append(shared.tile([P, P, PACK], BF16, name="gate_bf%d" % b, offset=(1 + 3 * b) * block_bytes // 2, align_bytes=64))
            interleave_w(nc.scalar.copy, gate_bf[b][:], gate_raw, row_blocks[b])
            w_codes[GATE, b] = sb.tile([P, P], U32, name="gate_codes%d" % b, align_bytes=64)
            w_scales[GATE, b] = sb.tile([P, P], U8, name="gate_scales%d" % b, align_bytes=64)
        quantize(w_codes[GATE, A][:], w_scales[GATE, A][:], gate_bf[A][:])
        quantize(x_codes[1][:], x_scales[1][:], x_bf[1][:])
        cand_bf = []
        for b in (A, B):
            cand_bf.append(shared.tile([P, P, PACK], BF16, name="cand_bf%d" % b, offset=b * block_bytes, align_bytes=64))
            interleave_w(nc.vector.tensor_copy, cand_bf[b][:], cand_raw, row_blocks[b])
            if b == A:
                quantize(w_codes[GATE, B][:], w_scales[GATE, B][:], gate_bf[B][:])
        for b in (A, B):
            cand_codes = sb.tile([P, P], U32, name="cand_codes%d" % b, align_bytes=64)
            cand_scales = sb.tile([P, P], U8, name="cand_scales%d" % b, align_bytes=64)
            quantize(cand_codes[:], cand_scales[:], cand_bf[b][:])
            w_codes[CAND, b], w_scales[CAND, b] = cand_codes[:], cand_scales[:]

        def activate(dst, func, codes, scales, cols, name):
            acc = ps.tile([P, S], F32, name=name)
            for h in range(2):
                if cols.start <= halves[h].start and halves[h].stop <= cols.stop:
                    nc.tensor.matmul_mx(
                        out=acc[:, halves[h]],
                        lhsT=codes.bitcast(FP8X4),
                        lhsT_scale=scales,
                        rhs=x_codes[h][:].bitcast(FP8X4),
                        rhs_scale=x_scales[h][:],
                        start=True,
                        stop=True,
                    )
            nc.scalar.activation(dst[:, cols], acc[:, cols], func, scale=-1.0)

        keep = [sb.tile([P, S], F32, name="keep%d" % b) for b in (A, B)]
        neg_cand = [sb.tile([P, S], F32, name="neg_cand%d" % b) for b in (A, B)]
        kept = [sb.tile([P, S], F32, name="kept%d" % b) for b in (A, B)]
        for b in (A, B):
            for h in range(2):
                activate(keep[b], ACT.Sigmoid, w_codes[GATE, b][:], w_scales[GATE, b][:], halves[h], "gate%d%d" % (b, h))
        for b in (A, B):
            for h in range(2):
                activate(neg_cand[b], ACT.Tanh, w_codes[CAND, b], w_scales[CAND, b], halves[h], "cand%d%d" % (b, h))

        def gated(dst, b, cols):
            nc.vector.scalar_tensor_tensor(dst[:, cols], keep[b][:, cols], 1.0, neg_cand[b][:, cols], ALU.subtract, ALU.mult)

        def look_up(b, cols):
            nc.vector.tensor_tensor(kept[b][:, cols], mem_t[b][:].indirect(entries(slot_t, cols)), keep[b][:, cols], ALU.mult)

        new_a = sb.tile([P, S], F32, name="new_a")
        old_b = sb.tile([P, OLD_SCALAR], F32, name="old_b")
        for cols in halves:
            look_up(A, cols)
        for cols in halves:
            gated(keep[A], A, cols)
        scalar_gather(old_b[:], mem_t[B][:].indirect(entries(slot_t, slice(0, OLD_SCALAR))))
        nc.vector.tensor_tensor(new_a[:, halves[0]], kept[A][:, halves[0]], keep[A][:, halves[0]], ALU.add)
        gated(neg_cand[A], B, whole)
        look_up(B, slice(OLD_SCALAR, S))
        nc.vector.tensor_tensor(kept[B][:, 0:OLD_SCALAR], old_b[:], keep[B][:, 0:OLD_SCALAR], ALU.mult)
        nc.vector.tensor_tensor(new_a[:, halves[1]], kept[A][:, halves[1]], keep[A][:, halves[1]], ALU.add)
        for cols in halves:
            nc.scalar.activation(mem_t[A][:].indirect(entries(slot_t, cols)), new_a[:, cols], ACT.Copy)
        nc.vector.tensor_tensor(mem_t[B][:].indirect(slot_t[:]), kept[B][:], neg_cand[A][:], ALU.add)
        nc.scalar.dma_start(out[row_blocks[A], :], mem_t[A][:])
        nc.sync.dma_start(out[row_blocks[B], :], mem_t[B][:])
